import numpy as np, ml_dtypes
CORES = [1,5,17,21,33,37,49,53]
N = 8
import mx_ref
BF = ml_dtypes.bfloat16
def gcols(t, e):
    v = np.concatenate([t.reshape(8, 16, -1, 4), np.zeros((8, 16, 1, 4), BF)], axis=2)
    return np.ascontiguousarray(np.stack([v[g][:, e[g]] for g in range(8)])).reshape(128, -1)
def tile(rs):
    return np.stack(rs, axis=2).reshape(128, -1).astype(BF)
def cut(t, i, w=512):
    return t[:, w * i:w * i + w]
def pick(q, e):
    c = np.concatenate([q[0].reshape(128, -1, 4), np.zeros((128, 1, 4), np.uint8)], axis=1); s = np.concatenate([q[1], np.ones((16, 1), np.uint8)], axis=1)
    return (np.ascontiguousarray(c[:, e].reshape(128, -1)), np.ascontiguousarray(s[:, e]))
def join(*qs):
    return (np.concatenate([q[0] for q in qs], axis=1), np.concatenate([q[1] for q in qs], axis=1))
def put(q, e, v):
    c, s = q[0].reshape(128, -1, 4).copy(), q[1].copy(); c[:, e] = v[0].reshape(128, -1, 4); s[:, e] = v[1]
    return (c.reshape(128, -1), s)
def pk(c, s):
    return (np.ascontiguousarray(c), mx_ref.live(s))
def emit(q):
    return q[0], q[1]
def packed(v, rng):
    q = [mx_ref.quantize(np.ascontiguousarray(v[r])) for r in range(N)]
    return np.stack([a for a, b in q]), np.stack([mx_ref.plane(b, rng) for a, b in q])
def values_of_codes():
    e, c = np.zeros((128, 128, 4), np.float32), np.zeros((128, 2, 4), np.uint8)
    e[np.arange(128), np.arange(128), 0] = 1
    c[:127, :, 0] = np.arange(256).reshape(2, 128).T[:127]
    return mx_ref.matmul(mx_ref.quantize(e.reshape(128, 512).astype(BF)), (c.reshape(128, 8), np.full((16, 2), 127, np.uint8))).T.reshape(-1).astype(np.float64)
CODE_VALUE, SCALE_VALUE = values_of_codes(), 2.0 ** (np.arange(256) - 127.0)
def decode(q):
    return (CODE_VALUE[q[0]].reshape(16, 8, -1, 4) * SCALE_VALUE[q[1]][:, None, :, None] + 0.0).reshape(128, -1).astype(np.float32)
def f(rng, *shape):
    return mx_ref.flush((rng.standard_normal(shape, dtype=np.float32) * np.exp2(rng.integers(-2, 3, shape[:-1] + (1,)))).astype(BF))
def wide(rng, *shape, cols=0):
    v = rng.standard_normal(shape, dtype=np.float32) * np.exp2(rng.integers(-12, 13, shape)).astype(np.float32)
    if cols: v *= np.repeat(np.exp2(rng.integers(-cols, cols + 1, shape[:-2] + (1, shape[-1] // 4))) * (rng.random(shape[:-2] + (1, shape[-1] // 4)) > 0.0625), 4, axis=-1).astype(np.float32)
    return mx_ref.flush(v.astype(BF))
C, K, R = 384, 96, 2
def choose(p):
    o = np.argsort(-(p[::16] + np.float32(0.0)), axis=1, kind="stable")
    return np.sort(o[:, :K], axis=1), np.sort(o[:, C - K:], axis=1)
def edit(hi, lo):
    e = []
    for g in range(8):
        stay = np.delete(np.arange(C), lo[g])
        key = np.concatenate([2 * stay, 2 * hi[g] + 1])
        e.append(np.concatenate([stay, C + np.arange(K)])[np.argsort(key)])
    return np.stack(e)
def numbers_of(rng):
    return {"x": np.array(f(rng, N, 128, 4 * C)), "u": np.array(f(rng, N, 128, 512)), "v": np.array(f(rng, N, 128, 512))}
def weights(rng, w, z):
    wc, ws = packed(w, rng)
    zc, zs = packed(z, rng)
    return {"wc": wc, "ws": ws, "zc": zc, "zs": zs}
def still(rng):
    w = np.zeros((N, 128, 4, 128, 4), np.float32)
    i = np.arange(128)
    for b in range(4): w[:, i, b, i, b] = 64
    return weights(rng, w.reshape(N, 128, 2048).astype(BF), np.zeros((N, 128, 2048), BF))
def signs(rng):
    return np.stack([rng.permutation(8) % 2 * 2.0 - 1.0 for r in range(N)])
def marks():
    n = np.arange(K)
    h = C - 2 * K
    v = np.ones((8, C), np.float32)
    cases = ((n, h + K + n), (h + K + n, n), (2 * n, 2 * n + 1), (2 * n + 1, 2 * n), (h + 2 * n, h + 2 * n + 1), (h + 2 * n + 1, h + 2 * n), (n, K + n), (K + n, n))
    for g in range(8):
        v[g, cases[g][0]] = 4
        v[g, cases[g][1]] = -2
    return v
def setup_inputs(rng):
    return {**numbers_of(rng), **weights(rng, f(rng, N, 128, 2048), f(rng, N, 128, 2048))}
def setup_inputs_ties(rng):
    d = numbers_of(rng)
    e = rng.permutation(N)
    x = d["x"].reshape(N, 8, 16, C, 4)
    for r in range(N):
        k = np.zeros(C, int) if r == e[0] else rng.permutation(C) % 3
        a = x[r][:, :8, :3].copy()
        a[:, :, 2] = 0
        x[r][:, :8] = a[:, :, k]
    x[e[1]] = 0
    u = d["u"].reshape(N, 8, 16, 128, 4)
    u[:, :, 8:, ::16] = 0
    w = np.array(f(rng, N, 128, 2048)).reshape(N, 8, 16, 4, 8, 16, 4)
    z = np.array(f(rng, N, 128, 2048)).reshape(N, 8, 16, 4, 8, 16, 4)
    for a in (w, z): a[:, :, 8:, :, :, :8] = 0
    return {"x": x.reshape(N, 128, 4 * C), "u": u.reshape(N, 128, 512), "v": d["v"], **weights(rng, w.reshape(N, 128, 2048), z.reshape(N, 128, 2048))}
def setup_inputs_ends(rng):
    d = numbers_of(rng)
    x = d["x"].reshape(N, 8, 16, C, 4)
    u = d["u"].reshape(N, 8, 16, 128, 4)
    x[:, :, 0] = 0
    u[:, :, :, ::16] = 0
    for r in range(N): x[r, :, 0, :, 0] = marks()[rng.permutation(8)].astype(BF)
    for g in range(8): u[:, g, 0, 16 * g, 0] = 1
    w = f(rng, N, 128, 2048).astype(np.float32).reshape(N, 8, 16, 4, 8, 16, 4)
    z = f(rng, N, 128, 2048).astype(np.float32).reshape(N, 8, 16, 4, 8, 16, 4)
    for a in (w, z):
        a[:, :, 15] = 0
        a[:, :, :, :, :, 15] *= np.float32(8192)
    return {**d, "x": x.reshape(N, 128, 4 * C), "u": u.reshape(N, 128, 512), **weights(rng, w.reshape(N, 128, 2048).astype(BF), z.reshape(N, 128, 2048).astype(BF))}
def setup_inputs_near(rng):
    d = numbers_of(rng)
    x = d["x"].astype(np.float32).reshape(N, 8, 16, C, 4)
    s = np.minimum((np.arange(C) + 1) // 2, 255)
    g = ((s[:, None] >> np.arange(8)) & 1) * np.exp2(np.arange(8) - 23.0)
    x[:, :, 0] = 0
    x[:, :, 0, :, 0] = signs(rng)[:, :, None]
    for r in rng.permutation(N)[:N // 2]:
        x[r, :, 0, C - 1, 0] = 16
        x[r, :, 0, 0, 0] = -16
    x[:, :, 8] = g[:, :4]
    x[:, :, 9] = g[:, 4:]
    x[:, :, 10:] = rng.integers(4, 8, (N, 8, 6, C, 4)) * rng.choice([-1.0, 1.0], (N, 8, 6, C, 4)) * 2.0 ** -20
    k = np.exp2(-1.0 * rng.permutation(np.arange(N) * 30 // (N - 1))).astype(np.float32).astype(BF)
    u = d["u"].reshape(N, 128, 128, 4)
    u[:, :, ::16] = 0
    for h in range(0, 128, 16):
        u[:, h, h, 0] = k
        u[:, h + 8:h + 10, h] = k[:, None, None]
    return {"x": x.reshape(N, 128, 4 * C).astype(BF), "u": u.reshape(N, 128, 512), "v": d["v"], **still(rng)}
def setup_inputs_huge(rng):
    d = numbers_of(rng)
    x = 2.0 ** 30 * (0.6 + 0.4 * rng.random((N, 128, C, 4)))
    c = np.stack([rng.permutation(C) % 2 * 2.0 - 1.0 for r in range(N)])
    c[rng.permutation(N) < N // 2] = 1
    x *= c[:, None, :, None]
    u = d["u"].reshape(N, 128, 128, 4)
    a = 2.0 ** 30 * (1 - 0.25 * rng.random((N, 128, 8, 4))) * signs(rng)[:, None, :, None]
    u[:, :, ::16] = a.astype(np.float32).astype(BF)
    return {"x": x.astype(np.float32).reshape(N, 128, 4 * C).astype(BF), "u": u.reshape(N, 128, 512), "v": d["v"], **still(rng)}
def setup_inputs_spread(rng):
    d = setup_inputs(rng)
    d["x"] = wide(rng, N, 128, 4 * C, cols=6)
    return d
def check_inputs(d):
    b = []
    for k in ("x", "u", "v"):
        a = np.abs(d[k].astype(np.float32))
        if not (np.isfinite(a).all() and ((a == 0) | (a >= 2.0 ** -30) & (a <= 2.0 ** 30)).all()): b.append("a value of " + k)
    return b
def reference(x, u, v, wc, ws, zc, zs):
    qu = [mx_ref.quantize(u[r]) for r in range(N)]
    w, z = [pk(wc[r], ws[r]) for r in range(N)], [pk(zc[r], zs[r]) for r in range(N)]
    now = [x[r] for r in range(N)]
    behind = (np.arange(C) + 1) % C
    ol = np.zeros((N, 8, C), np.float32)
    for t in range(R):
        hi, lo, border = [], [], []
        for r in range(N):
            h, l = choose(mx_ref.matmul(qu[r], mx_ref.quantize(now[r])))
            hi.append(h)
            lo.append(l)
            border.append(mx_ref.quantize(gcols(now[r], l)))
        came = decode(join(*border)).astype(BF)
        for r in range(N):
            a = (r - 1) % N
            e = edit(hi[r], lo[r])
            q = mx_ref.quantize(gcols(np.concatenate([now[r], cut(came, a, 4 * K)], axis=1), e))
            made = []
            for b in range(4):
                c = np.arange(128 * b, 128 * b + 128)
                made.append((mx_ref.matmul(pick(w[r], c), q) + mx_ref.matmul(pick(z[r], c), q)[:, behind]) * np.float32(0.015625))
            now[r] = tile(made)
            ol[r] = np.take_along_axis(np.concatenate([np.tile(np.arange(C), (8, 1)), C + lo[a]], axis=1), e, axis=1)
    y = np.zeros((N, 128, C), np.float32)
    oc, osc = np.zeros((N, 128, 4 * C), np.uint8), np.zeros((N, 16, C), np.uint8)
    for r in range(N):
        q = mx_ref.quantize(now[r])
        y[r] = mx_ref.matmul(mx_ref.quantize(v[r]), q)
        oc[r], osc[r] = emit(q)
    return {"y": y, "ol": ol, "oc": oc, "osc": osc}

@@ -1,0 +1,456 @@
+from concourse.mybir import dt, AluOpType, ActivationFunctionType
+
+C, K, R = 384, 96, 2
+H = C // 2
+NB = C // 16
+OFF = 240
+HOLE = 250.0
+TILES = [(384, ["a", "b", 23, 22]), (336, [21, 20, 19, 18]), (272, [17, 16, 15, 14]), (208, [13, 12, 11, 10]),
+         (144, [9, 8, 7, 6]), (128, [1]), (128, [5, 4, 3, 2])]
+
+BF, F32, F16, I32, U16, U8, X4 = "bfloat16", "float32", "float16", "int32", "uint16", "uint8", "float8_e4m3fn_x4"
+
+
+def _sb(n, d):
+    return ("sbuf", [128, n], d)
+
+
+SCRATCH = {
+    "xc0": _sb(4 * (C + K), BF), "xc1": _sb(4 * (C + K), BF), "xc2": _sb(4 * C, BF),
+    "ub": _sb(512, BF), "vb": _sb(512, BF),
+    "uq": _sb(128, X4), "us": _sb(128, U8), "upq": _sb(128, X4), "ups": _sb(128, U8),
+    "vq": _sb(128, X4), "vs": _sb(128, U8),
+    "wq": _sb(512, X4), "wsc": _sb(512, U8), "zq": _sb(512, X4), "zsc": _sb(512, U8),
+    "xq": _sb(C, X4), "xs": _sb(C, U8),
+    "zb": _sb(512, BF), "ones": _sb(128, BF), "unit": _sb(528, BF),
+    "eq": _sb(512, X4), "es": _sb(512, U8),
+    "onb": _sb(512, BF), "onq": _sb(128, X4), "ons": _sb(128, U8),
+    "dtb": _sb(512, BF), "dtq": _sb(128, X4), "dts": _sb(128, U8),
+    "pi": _sb(1, I32), "ci": _sb(4, I32), "cf": _sb(4, F32), "c4": _sb(1, F32),
+    "m4": _sb(128, BF), "l16": _sb(NB, I32), "ulist": _sb(8, U16), "plist": _sb(NB, U16),
+    "k16": _sb(C, BF), "k4": _sb(C, BF), "mask16": _sb(C, BF), "keep16": _sb(C, BF), "mask4": _sb(C, BF), "keep4": _sb(C, BF),
+    "gate4": _sb(K, BF), "cab": _sb(2 * NB, F32), "jc": _sb(NB, F32), "jv": _sb(C, BF),
+    "m1": _sb(C, F32), "sc": _sb(C, F32), "pex": _sb(C, F32), "junk": _sb(8 * NB * (NB - 1), BF),
+    "rs": _sb(NB, F32), "ab": _sb(2 * NB, F32), "m2": _sb(C, F16), "sc2": _sb(C, F16),
+    "ft": _sb(512, BF), "fq": _sb(128, X4), "fs": _sb(128, U8), "hi": _sb(NB, F32),
+    "pre": _sb(2 * NB, F32), "inc": _sb(2 * NB, F32), "x1": _sb(2 * NB, F32), "nm": _sb(2 * NB, F32),
+    "dst": _sb(NB, F32), "doff": _sb(NB, U16),
+    "win0": _sb(C + K, BF), "win1": _sb(C + K, BF),
+    "bsn": _sb(K, BF), "boff": _sb(NB, U16), "bt": _sb(512, BF),
+    "bq0": _sb(128, X4), "bs0": _sb(128, U8), "bq1": _sb(128, X4), "bs1": _sb(128, U8),
+    "lq": _sb(2 * K + 128, X4), "ls": _sb(2 * K + 128, U8), "ll": _sb(K, BF),
+    "hole": _sb(C, BF), "hs": _sb(C, BF), "ee": _sb(C, BF), "em": _sb(C, BF), "esn": _sb(C, BF), "toff": _sb(K + 2, U16),
+    "tt": _sb(4 * C + 16, BF), "tq": _sb(C, X4), "ts": _sb(C, U8), "rq": _sb(C, X4), "rsc": _sb(C, U8),
+    "om": _sb(C, BF), "osn": _sb(C, BF), "ooff": _sb(NB, U16), "ow": _sb(C + K, F32), "ob": _sb(C, F32),
+    "yb": _sb(C, F32),
+}
+for _i, (_n, _p) in enumerate(TILES):
+    SCRATCH["f%d" % _i] = _sb(4 * _n, BF)
+    SCRATCH["fq%d" % _i] = _sb(_n, X4)
+    SCRATCH["fs%d" % _i] = _sb(_n, U8)
+for _i in range(8):
+    SCRATCH["ps%d" % _i] = ("psum", [128, 512], F32)
+
+SEMAPHORES = ["sV", "sS", "sP", "sG", "ldu", "ldx0", "ldx1", "ldw", "ldv", "arr0", "arr1", "arrl", "sent", "outs"]
+
+
+def rank_program(g, core, T, topo):
+    rank = T.rank_of(core)
+    if rank is None:
+        return
+    A, AF = AluOpType, ActivationFunctionType
+    n = len(T.cores)
+    nxt, prv = T.cores[(rank + 1) % n], T.cores[(rank - 1) % n]
+
+    def lanes(src, dst):
+        e = topo.engines(src, dst)
+        return e[::max(1, len(e) // 8)]
+
+    out_e, in_e = lanes(core, nxt), lanes(prv, core)
+    out_mask = sum(1 << e for e in out_e)
+    rid, pid = topo.addr(nxt)[:2]
+
+    Q = {"V": g.vector, "S": g.scalar, "P": g.tensor, "G": g, "Y": g.sync}
+    cnt = {"V": 0, "S": 0, "P": 0, "G": 0}
+    known = {e: {} for e in Q}
+    writer, readers = {}, {}
+    total = {"sent": 0, "outs": 0}
+
+    def need(e, tok):
+        sem, val, clock = tok[0], tok[1], tok[2]
+        if known[e].get(sem, 0) < val:
+            Q[e].wait_ge(T.sem[sem], val)
+            for s, v in clock.items():
+                known[e][s] = max(known[e].get(s, 0), v)
+
+    def order(e, r, w):
+        toks = []
+        for k in r:
+            if k in writer:
+                toks.append(writer[k])
+            if k.startswith("ps"):
+                toks += [t for t in readers.get(k, []) if t[3] != e]
+        for k in w:
+            if k in writer and not (e == "P" and writer[k][3] == "P"):
+                toks.append(writer[k])
+            toks += readers.get(k, [])
+        best = {}
+        for t in toks:
+            if t[0] not in best or best[t[0]][1] < t[1]:
+                best[t[0]] = t
+        for t in sorted(best.values(), key=lambda t: -len(t[2])):
+            need(e, t)
+
+    def note(tok, r, w):
+        for k in r:
+            readers.setdefault(k, []).append(tok)
+        for k in w:
+            writer[k] = tok
+            readers[k] = []
+
+    def op(e, call, r=(), w=()):
+        order(e, r, w)
+        cnt[e] += 1
+        call().then_inc(T.sem["s" + e], 1)
+        clock = dict(known[e])
+        clock["s" + e] = cnt[e]
+        note(("s" + e, cnt[e], clock, e), r, w)
+
+    def dma(e, out, in_, sem, val, r=(), w=()):
+        order(e, r, w)
+        Q[e].dma_start(out, in_).then_inc(T.sem[sem], 16)
+        clock = dict(known[e])
+        clock[sem] = val
+        note((sem, val, clock, "D"), r, w)
+
+    def store(e, out, in_, r):
+        order(e, r, ())
+        Q[e].dma_start(out, in_).then_inc(T.sem.outs, 16)
+        total["outs"] += 16
+
+    def send(out, in_, sem, r):
+        order("G", r, ())
+        g.remote_dma(out, in_, T.sem[sem], T.sem.sent, pid, rid, out_mask)
+        total["sent"] += len(out_e)
+
+    def arrival(key, sem, writes):
+        writer[key] = (sem, writes * len(in_e), {sem: writes * len(in_e)}, "D")
+
+    V, S = g.vector, g.scalar
+
+    def ts(out, in0, s1, o0, s2=None, o1=None, r=(), w=()):
+        if o1 is None:
+            op("V", lambda: V.tensor_scalar(out, in0, s1, None, o0), r, w)
+        else:
+            op("V", lambda: V.tensor_scalar(out, in0, s1, s2, o0, o1), r, w)
+
+    def tt(out, a, b, o, r, w):
+        op("V", lambda: V.tensor_tensor(out, a, b, o), r, w)
+
+    def scan(out, a, b, init, o0, o1, r, w):
+        op("V", lambda: V.tensor_tensor_scan(out, a, b, init, o0, o1), r, w)
+
+    def vcopy(out, in_, r, w):
+        op("V", lambda: V.tensor_copy(out, in_), r, w)
+
+    def fill(out, val, w):
+        op("V", lambda: V.memset(out, val), (), w)
+
+    def quant(q, s, in_, r, w):
+        op("V", lambda: V.quantize_mx(q, s, in_), r, w)
+
+    def act(out, in_, f, r, w, **kw):
+        op("S", lambda: S.activation(out, in_, f, **kw), r, w)
+
+    def mm(out, lq, ls, rq, rs, start, stop, r, w):
+        op("P", lambda: g.tensor.matmul_mx(out, lq, ls, rq, rs, start, stop), r, w)
+
+    def iota(out, pattern, base, mult, w, small=True):
+        if small:
+            op("G", lambda: g.iota(out, pattern, base, mult, allow_small_or_imprecise_dtypes=True), (), w)
+        else:
+            op("G", lambda: g.iota(out, pattern, base, mult), (), w)
+
+    def asel(out, in_, pattern, cmp, base, mult, r, w):
+        op("G", lambda: g.affine_select(out, in_, pattern, cmp, 0.0, base, mult), r, w)
+
+    def four(name):
+        return ["%s.%d" % (name, t) for t in range(4)]
+
+    PS = [T["ps%d" % i] for i in range(8)]
+    XC = [T.xc0, T.xc1, T.xc2]
+
+    def xk(t, h):
+        return ["x%d.%d.%d" % (t, h, b) for b in range(4)]
+
+    dma("Y", T.ub[:], T.u[:], "ldu", 16, w=["ub"])
+    dma("S", T.xc0[:, 0:4 * H], T.x[:, 0:4 * H], "ldx0", 16, w=xk(0, 0))
+    dma("Y", T.xc0[:, 4 * H:4 * C], T.x[:, 4 * H:4 * C], "ldx1", 16, w=xk(0, 1))
+    order("Y", xk(0, 0) + xk(0, 1), ())
+    g.sync.dma_start(T.wq[:].bitcast(dt.uint8), T.wc[:]).then_inc(T.sem.ldw, 16)
+    g.sync.dma_start(T.zq[:].bitcast(dt.uint8), T.zc[:]).then_inc(T.sem.ldw, 16)
+    g.sync.dma_start(T.wsc[:], T.ws[:]).then_inc(T.sem.ldw, 16)
+    dma("Y", T.zsc[:], T.zs[:], "ldw", 64, w=["wz"])
+    dma("Y", T.vb[:], T.v[:], "ldv", 16, w=["vb"])
+
+    iota(T.pi[:], [[0, 1]], 0, 1, ["pi"], small=False)
+    iota(T.l16[:], [[16, NB]], 0, 0, ["l16"], small=False)
+    iota(T.k16[:], [[0, NB], [1, 16]], 0, 0, ["k16"])
+    iota(T.m4[:], [[1, 8], [0, 16]], 0, 0, ["m4"])
+    fill(T.zb[:], 0.0, ["zb"])
+    ts(T.ci[:, 0:1], T.pi[:], 4, A.arith_shift_right, r=["pi"], w=["ci0"])
+    ts(T.ci[:, 1:2], T.pi[:], 15, A.bitwise_and, r=["pi"], w=["ci1"])
+    ts(T.ci[:, 2:3], T.pi[:], 2, A.arith_shift_right, 3, A.bitwise_and, r=["pi"], w=["ci2"])
+    ts(T.ci[:, 3:4], T.pi[:], 3, A.bitwise_and, r=["pi"], w=["ci3"])
+    vcopy(T.ulist[:], T.l16[:, 0:8], ["l16"], ["ulist"])
+    vcopy(T.cf[:], T.ci[:], ["ci0", "ci1", "ci2", "ci3"], ["cf"])
+    ts(T.plist[:], T.l16[:], 15.0, A.add, r=["l16"], w=["plist"])
+    fill(T.rs[:, 0:1], 0.0, ["rs0"])
+    fill(T.ones[:], 1.0, ["ones"])
+    ts(T.c4[:], T.cf[:, 3:4], 4.0 * OFF, A.add, r=["cf"], w=["c4"])
+    ts(T.jc[:], T.l16[:], T.cf[:, 1:2], A.add, -float(K), A.add, r=["l16", "cf"], w=["jc"])
+    fill(T.unit[:], 0.0, ["unit"])
+    ts(T.mask16[:], T.k16[:], T.cf[:, 1:2], A.is_equal, r=["k16", "cf"], w=["mask16"])
+    ts(T.onb[:, 0:512:4], T.m4[:], T.cf[:, 0:1], A.is_equal, r=["m4", "cf"], w=["onb.0"])
+    fill(T.win0[:], HOLE, ["win0"])
+
+    def zero(i):
+        cols, planes = TILES[i]
+        a = 4 * 16 * min(p for p in planes if not isinstance(p, str)) if len(planes) == 4 else 0
+        act(T["f%d" % i][:, a:4 * cols], T.zb[:, 0:4 * cols - a], AF.Copy, ["zb"], four("f%d" % i))
+
+    zero(4)
+    zero(6)
+    zero(3)
+    act(T.keep16[:], T.k16[:], AF.Sign, ["k16"], ["keep16"])
+    for t in (1, 2, 3):
+        act(T.onb[:, t:512:4], T.onb[:, 0:512:4], AF.Copy, ["onb.0"], ["onb.%d" % t])
+    asel(T.dtb[:, 0:512:4], T.onb[:, 0:512:4], [[1, 128]], A.is_gt, 0, -1, ["onb.0"], ["dtb.0"])
+    asel(T.dtb[:, 1:512:4], T.onb[:, 0:512:4], [[-1, 128]], A.is_gt, 0, 1, ["onb.0"], ["dtb.1"])
+    asel(T.unit[:, 3:515:4], T.ones[:], [[-1, 128]], A.is_equal, 0, 1, ["ones"], ["unit"])
+    iota(T.k4[:], [[0, K], [1, 4]], 0, 0, ["k4"])
+    iota(T.cab[:], [[C - 2 * K + 1, 2], [-16, NB]], K - 1, 0, ["cab"])
+    iota(T.jv[:], [[1, C]], -OFF, 0, ["jv"])
+    iota(T.ow[:, 0:C], [[1, C]], 0, 0, ["ow0"])
+    quant(T.uq[:], T.us[:], T.ub[:], ["ub"], ["uq"])
+    act(T.ups[:], T.us[:].indirect(T.ulist[:]), AF.Copy, ["uq", "ulist"], ["ups"])
+    vcopy(T.upq[:].bitcast(dt.uint32), T.uq[:].bitcast(dt.uint32).indirect(T.ulist[:]), ["uq", "ulist"], ["upq"])
+    zero(5)
+    for t in (2, 3):
+        act(T.dtb[:, t:512:4], T.onb[:, 0:512:4], AF.Copy, ["onb.0"], ["dtb.%d" % t])
+    for i in (0, 1, 2):
+        zero(i)
+
+    def quant_state(t, h):
+        quant(T.xq[:, h * H:h * H + H], T.xs[:, h * H:h * H + H], XC[t][:, 4 * h * H:4 * h * H + 4 * H], xk(t, h), ["xq%d" % h])
+
+    def scores(bank, cols):
+        mm(PS[bank][:, 0:cols], T.upq[:], T.ups[:], T.xq[:, 0:cols], T.xs[:, 0:cols], True, True,
+           ["upq", "ups", "xq0"] + (["xq1"] if cols > H else []), ["ps%d" % bank])
+
+    def pivots(h):
+        a = h * H
+        tt(T.m1[:, a:a + H], PS[h][:, a:a + H], T.mask16[:, a:a + H], A.mult, ["ps%d" % h, "mask16"], ["m1%d" % h])
+        return lambda: scan(T.sc[:, a:a + H], T.keep16[:, a:a + H], T.m1[:, a:a + H], 0.0, A.mult, A.add, ["keep16", "m1%d" % h], ["sc%d" % h])
+
+    def plane(p):
+        i, s = [(i, pl.index(p)) for i, (c, pl) in enumerate(TILES) if p in pl][0]
+        F, key = T["f%d" % i], "f%d.%d" % (i, s)
+        if isinstance(p, str):
+            tt(F[:, s:4 * C:4], T.pex[:], PS[1][:, 0:C], A.is_lt if p == "a" else A.is_le, ["pex", "ps1"], [key])
+        else:
+            h = 16 * p // H
+            ts(F[:, s:64 * p:4], PS[h][:, 0:16 * p], T.sc[:, 16 * p + 15:16 * p + 16], A.is_ge, r=["ps%d" % h, "sc%d" % h], w=[key])
+            a = 8 * p * (p - 1)
+            act(T.junk[:, a:a + 16 * p], F[:, s:64 * p:4], AF.Copy, [key], ["rs%d" % p], accum_out=T.rs[:, p:p + 1])
+
+    def pack(i):
+        quant(T["fq%d" % i][:], T["fs%d" % i][:], T["f%d" % i][:], four("f%d" % i), ["qf%d" % i])
+
+    def columns(i):
+        sq, ss, sk = (T.dtq, T.dts, "dtq") if i == 0 else (T.onq, T.ons, "onq")
+        mm(PS[2][:, 0:TILES[i][0]], sq[:], ss[:], T["fq%d" % i][:], T["fs%d" % i][:], i == 0, i == 3, [sk, "qf%d" % i], ["ps2"])
+
+    quant_state(0, 0)
+    scores(0, H)
+    quant_state(0, 1)
+    scores(1, C)
+
+    for t in range(R):
+        last = t == R - 1
+        X, win, wk = XC[t], T["win%d" % t], "win%d" % t
+        xall = xk(t, 0) + xk(t, 1)
+        rest = pivots(0)
+        if t == 0:
+            quant(T.onq[:], T.ons[:], T.onb[:], four("onb"), ["onq"])
+        rest()
+        for p in (9, 8, 7, 6):
+            plane(p)
+        if t > 0:
+            quant_state(t, 1)
+            scores(1, C)
+        pack(4)
+        for p in (11, 10, 5, 4, 3, 2):
+            plane(p)
+        rest = pivots(1)
+        pack(6)
+        rest()
+        plane(1)
+        act(T.pex[:], T.sc[:].indirect(T.plist[:]), AF.Copy, ["sc0", "sc1", "plist"], ["pex"])
+        for p in (23, 22, 21, 20, 19, 18, "a", "b"):
+            plane(p)
+        if t == 0:
+            quant(T.dtq[:], T.dts[:], T.dtb[:], four("dtb"), ["dtq"])
+        pack(5)
+        pack(0)
+        for p in (17, 16, 15, 14):
+            plane(p)
+        pack(1)
+        for i in (0, 4, 6, 5, 1):
+            columns(i)
+        for p in (13, 12):
+            plane(p)
+        pack(2)
+        columns(2)
+        pack(3)
+        columns(3)
+        if t == 0:
+            act(T.ft[:], T.zb[:], AF.Copy, ["zb"], ["ft.lo", "ft.hl"])
+            act(T.keep4[:], T.k4[:], AF.Sign, ["k4"], ["keep4"])
+            act(T.bt[:, C:512], T.zb[:, 0:512 - C], AF.Copy, ["zb"], ["bt.z"])
+            ts(T.mask4[:], T.k4[:], T.cf[:, 2:3], A.is_equal, r=["k4", "cf"], w=["mask4"])
+        else:
+            fill(win[:], HOLE, [wk])
+        tt(T.m2[:], PS[2][:, 0:C], T.mask16[:], A.mult, ["ps2", "mask16"], ["m2"])
+        rsk = ["rs%d" % p for p in range(NB)]
+        tt(T.ab[:, 0:NB], T.rs[:], T.cab[:, 0:NB], A.add, rsk + ["cab"], ["ab0"])
+        scan(T.sc2[:], T.keep16[:], T.m2[:], 0.0, A.mult, A.add, ["keep16", "m2"], ["sc2"])
+        tt(T.ab[:, NB:2 * NB], T.rs[:], T.cab[:, NB:2 * NB], A.add, rsk + ["cab"], ["ab1"])
+        cs = T.sc2[:, 15:C:16]
+        lo = T.ft[:, 1:4 * NB:4]
+        tt(T.hi[:], T.ab[:, NB:2 * NB], cs, A.is_le, ["ab1", "sc2"], ["hi"])
+        tt(lo, T.ab[:, 0:NB], cs, A.is_ge, ["ab0", "sc2"], ["ft.lo"])
+        tt(T.ft[:, 4 * NB + 1:8 * NB:4], T.hi[:], lo, A.subtract, ["hi", "ft.lo"], ["ft.hl"])
+        quant(T.fq[:], T.fs[:], T.ft[:], ["ft.lo", "ft.hl"], ["fq"])
+        mm(PS[3][:, 0:128], T.onq[:], T.ons[:], T.fq[:], T.fs[:], True, True, ["onq", "fq"], ["ps3"])
+        mm(PS[0][:, 0:128], T.dtq[:], T.dts[:], T.fq[:], T.fs[:], True, True, ["dtq", "fq"], ["ps0"])
+        ts(T.pre[:, 0:NB], lo, 1000.0, A.mult, C - 1 - 1000.0, A.add, r=["ft.lo"], w=["pre0"])
+        tt(T.pre[:, NB:2 * NB], T.jc[:], T.hi[:], A.subtract, ["jc", "hi"], ["pre1"])
+        if t == 0:
+            ts(T.gate4[:], T.mask4[:, 0:K], 2000.0, A.mult, -1000.0, A.add, r=["mask4"], w=["gate4"])
+        else:
+            quant(T.vq[:], T.vs[:], T.vb[:], ["vb"], ["vq"])
+        scan(T.inc[:], PS[3][:, 0:2 * NB], T.zb[:, 0:2 * NB], 0.0, A.add, A.add, ["ps3", "zb"], ["inc"])
+        tt(T.x1[:], T.pre[:], PS[0][:, 0:2 * NB], A.subtract, ["pre0", "pre1", "ps0"], ["x1"])
+        tt(T.nm[:], T.x1[:], T.inc[:], A.add, ["x1", "inc"], ["nm"])
+        tt(T.dst[:], T.nm[:, 0:NB], T.nm[:, NB:2 * NB], A.max, ["nm"], ["dst"])
+        vcopy(T.doff[:], T.dst[:], ["dst"], ["doff"])
+        vcopy(win[:].indirect(T.doff[:]), T.jv[:], ["jv", "doff"], [wk])
+        if last:
+            send(T.ll[:], win[:, C:C + K], "arrl", [wk])
+            arrival("ll", "arrl", 1)
+        scan(T.bsn[:], T.gate4[:], win[:, C:C + K], 0.0, A.max, A.min, ["gate4", wk], ["bsn"])
+        ts(T.boff[:], T.bsn[:, 3:K:4], 4.0, A.mult, T.c4[:], A.add, r=["bsn", "c4"], w=["boff"])
+        act(T.bt[:, 2 * K:4 * K], X[:, 0:4 * C].indirect(T.boff[:, NB // 2:NB]), AF.Copy, xall + ["boff"], ["bt.1"])
+        vcopy(T.bt[:, 0:2 * K], X[:, 0:4 * C].indirect(T.boff[:, 0:NB // 2]), xall + ["boff"], ["bt.0"])
+        bq, bs = T["bq%d" % t], T["bs%d" % t]
+        quant(bq[:], bs[:], T.bt[:], ["bt.0", "bt.1", "bt.z"], ["bq%d" % t])
+        land = t * (K + 128)
+        send(T.lq[:, land:land + K].bitcast(dt.uint8), bq[:, 0:K].bitcast(dt.uint8), "arr%d" % t, ["bq%d" % t])
+        send(T.ls[:, land:land + K], bs[:, 0:K], "arr%d" % t, ["bq%d" % t])
+        arrival("land%d" % t, "arr%d" % t, 2)
+        if t == 0:
+            quant(T.lq[:, K:K + 128], T.ls[:, K:K + 128], T.zb[:], ["zb"], ["lfill"])
+            for b in range(4):
+                quant(T.eq[:, 128 * b:128 * b + 128], T.es[:, 128 * b:128 * b + 128], T.unit[:, 3 - b:515 - b], ["unit"], ["eq%d" % b])
+        ts(T.hole[:], win[:, 0:C], 200.0, A.is_gt, r=[wk], w=["hole"])
+        scan(T.hs[:], T.hole[:], T.zb[:, 0:C], float(C - 1 - OFF), A.add, A.add, ["hole", "zb"], ["hs"])
+        tt(T.ee[:], win[:, 0:C], T.hs[:], A.min, [wk, "hs"], ["ee"])
+        tt(T.em[:], T.ee[:], T.mask4[:], A.mult, ["ee", "mask4"], ["em"])
+        scan(T.esn[:], T.keep4[:], T.em[:], 0.0, A.mult, A.add, ["keep4", "em"], ["esn"])
+        ts(T.toff[:, 0:K], T.esn[:, 3:C:4], 4.0, A.mult, T.c4[:], A.add, r=["esn", "c4"], w=["toff0"])
+        ts(T.toff[:, K:K + 1], T.esn[:, 3:4], 4.0, A.mult, T.c4[:], A.add, r=["esn", "c4"], w=["toff1"])
+        if last:
+            act(T.ow[:, C:C + K], T.ll[:], AF.Identity, ["ll"], ["ow1"], bias=float(C + OFF))
+        view, first = (0, 0) if t == 0 else (land + K - 128, 128 - K)
+        for b in range(4):
+            mm(PS[4 + b][:, 0:128], T.eq[:, 128 * b:128 * b + 128], T.es[:, 128 * b:128 * b + 128],
+               T.lq[:, view:view + 128], T.ls[:, view:view + 128], True, True, ["eq%d" % b, "lfill", "land%d" % t], ["ps%d" % (4 + b)])
+        for b in range(4):
+            o, i_ = X[:, 4 * C + b:4 * (C + K):4], PS[4 + b][:, first:first + K]
+            if b < 3:
+                act(o, i_, AF.Copy, ["ps%d" % (4 + b)], ["came%d" % b])
+            else:
+                vcopy(o, i_, ["ps%d" % (4 + b)], ["came%d" % b])
+        src = xall + ["came%d" % b for b in range(4)] + ["toff0", "toff1"]
+        cut = [0, 24, 50, 66, K + 1]
+
+        def pick(e, k):
+            o, i_ = T.tt[:, 16 * cut[k]:16 * cut[k + 1]], X[:].indirect(T.toff[:, cut[k]:cut[k + 1]])
+            if e == "V":
+                vcopy(o, i_, src, ["tt%d" % k])
+            else:
+                act(o, i_, AF.Copy, src, ["tt%d" % k])
+
+        def quant_t(h, keys):
+            a = h * H
+            quant(T.tq[:, a:a + H], T.ts[:, a:a + H], T.tt[:, 4 * a:4 * a + 4 * H], keys, ["tq%d" % h])
+            quant(T.rq[:, a:a + H], T.rsc[:, a:a + H], T.tt[:, 4 * a + 4:4 * a + 4 * H + 4], keys, ["rq%d" % h])
+
+        steps = ((0, 0), (0, 1), (1, 0), (1, 1), (0, 2), (1, 2), (0, 3), (1, 3))
+
+        def layer(h, part):
+            a = h * H
+            for z, b in part:
+                wq, ws, mq, ms, mk = (T.zq, T.zsc, T.rq, T.rsc, "rq%d" % h) if z else (T.wq, T.wsc, T.tq, T.ts, "tq%d" % h)
+                mm(PS[4 * h + b][:, 0:H], wq[:, 128 * b:128 * b + 128], ws[:, 128 * b:128 * b + 128],
+                   mq[:, a:a + H], ms[:, a:a + H], z == 0, z == 1, ["wz", mk], ["ps%d" % (4 * h + b)])
+
+        def new_state(e, h, b):
+            o, i_ = XC[t + 1][:, 4 * h * H + b:4 * h * H + 4 * H:4], PS[4 * h + b][:, 0:H]
+            r, w = ["ps%d" % (4 * h + b)], [xk(t + 1, h)[b]]
+            if e == "V":
+                ts(o, i_, 0.015625, A.mult, r=r, w=w)
+            else:
+                act(o, i_, AF.Copy, r, w, scale=0.015625)
+
+        pick("S", 1)
+        pick("V", 0)
+        quant_t(0, ["tt0", "tt1"])
+        layer(0, steps)
+        pick("S", 3)
+        pick("V", 2)
+        quant_t(1, ["tt1", "tt2", "tt3"])
+        new_state("S", 0, 0)
+        new_state("V", 0, 1)
+        new_state("S", 0, 2)
+        new_state("V", 0, 3)
+        quant_state(t + 1, 0)
+        layer(1, steps[:4])
+        if not last:
+            scores(0, H)
+        layer(1, steps[4:])
+        for b in range(4):
+            new_state("S", 1, b)
+
+    store("Y", T.oc[:, 0:4 * H], T.xq[:, 0:H].bitcast(dt.uint8), ["xq0"])
+    mm(PS[0][:, 0:H], T.vq[:], T.vs[:], T.xq[:, 0:H], T.xs[:, 0:H], True, True, ["vq", "xq0"], ["ps0"])
+    tt(T.om[:], T.ee[:], T.mask16[:], A.mult, ["ee", "mask16"], ["om"])
+    scan(T.osn[:], T.keep16[:], T.om[:], 0.0, A.mult, A.add, ["keep16", "om"], ["osn"])
+    quant_state(R, 1)
+    mm(PS[1][:, 0:H], T.vq[:], T.vs[:], T.xq[:, H:C], T.xs[:, H:C], True, True, ["vq", "xq1"], ["ps1"])
+    act(T.yb[:, 0:H], PS[0][:, 0:H], AF.Copy, ["ps0"], ["yb0"])
+    ts(T.ooff[:], T.osn[:, 15:C:16], float(OFF), A.add, r=["osn"], w=["ooff"])
+    store("Y", T.y[:, 0:H], T.yb[:, 0:H], ["yb0"])
+    store("Y", T.oc[:, 4 * H:4 * C], T.xq[:, H:C].bitcast(dt.uint8), ["xq1"])
+    for k in range(4):
+        store("Y", T.osc[4 * k:4 * k + 4, :], T.xs[32 * k:32 * k + 4, :], ["xq0", "xq1"])
+    act(T.yb[:, H:C], PS[1][:, 0:H], AF.Copy, ["ps1"], ["yb1"])
+    vcopy(T.ob[:], T.ow[:].indirect(T.ooff[:]), ["ow0", "ow1", "ooff"], ["ob"])
+    store("S", T.y[:, H:C], T.yb[:, H:C], ["yb1"])
+    store("Y", T.ol[:], T.ob[0:128:16, :], ["ob"])
+
+    for e in ("V", "S", "P", "G"):
+        g.wait_ge(T.sem["s" + e], cnt[e])
+    g.wait_ge(T.sem.sent, total["sent"])
+    g.wait_ge(T.sem.outs, total["outs"])

@@ -3,10 +3,14 @@ from concourse.mybir import dt, AluOpType, ActivationFunctionType
 C, K, R = 384, 96, 2
 H = C // 2
 NB = C // 16
+HB = NB // 2
 OFF = 240
-HOLE = 250.0
-TILES = [(384, ["a", "b", 23, 22]), (336, [21, 20, 19, 18]), (272, [17, 16, 15, 14]), (208, [13, 12, 11, 10]),
-         (144, [9, 8, 7, 6]), (128, [1]), (128, [5, 4, 3, 2])]
+HOLE = 1024.0
+BIG = 9.0e29
+U = 1.0 / 512
+LOW = 512 - K
+TW = 49
+ON_S = (((), (11, 10)), ((), (11, 10)))
 
 BF, F32, F16, I32, U16, U8, X4 = "bfloat16", "float32", "float16", "int32", "uint16", "uint8", "float8_e4m3fn_x4"
 
@@ -22,32 +26,38 @@ SCRATCH = {
     "vq": _sb(128, X4), "vs": _sb(128, U8),
     "wq": _sb(512, X4), "wsc": _sb(512, U8), "zq": _sb(512, X4), "zsc": _sb(512, U8),
     "xq": _sb(C, X4), "xs": _sb(C, U8),
-    "zb": _sb(512, BF), "ones": _sb(128, BF), "unit": _sb(528, BF),
+    "zb": _sb(520, BF), "unit": _sb(520, BF),
     "eq": _sb(512, X4), "es": _sb(512, U8),
     "onb": _sb(512, BF), "onq": _sb(128, X4), "ons": _sb(128, U8),
     "dtb": _sb(512, BF), "dtq": _sb(128, X4), "dts": _sb(128, U8),
-    "pi": _sb(1, I32), "ci": _sb(4, I32), "cf": _sb(4, F32), "c4": _sb(1, F32),
-    "m4": _sb(128, BF), "l16": _sb(NB, I32), "ulist": _sb(8, U16), "plist": _sb(NB, U16),
-    "k16": _sb(C, BF), "k4": _sb(C, BF), "mask16": _sb(C, BF), "keep16": _sb(C, BF), "mask4": _sb(C, BF), "keep4": _sb(C, BF),
-    "gate4": _sb(K, BF), "cab": _sb(2 * NB, F32), "jc": _sb(NB, F32), "jv": _sb(C, BF),
-    "m1": _sb(C, F32), "sc": _sb(C, F32), "pex": _sb(C, F32), "junk": _sb(8 * NB * (NB - 1), BF),
-    "rs": _sb(NB, F32), "ab": _sb(2 * NB, F32), "m2": _sb(C, F16), "sc2": _sb(C, F16),
-    "ft": _sb(512, BF), "fq": _sb(128, X4), "fs": _sb(128, U8), "hi": _sb(NB, F32),
-    "pre": _sb(2 * NB, F32), "inc": _sb(2 * NB, F32), "x1": _sb(2 * NB, F32), "nm": _sb(2 * NB, F32),
+    "onu": _sb(128, BF), "tri": _sb(520, BF), "s1q": _sb(128, X4), "s1s": _sb(128, U8),
+    "s2q": _sb(128, X4), "s2s": _sb(128, U8),
+    "pi": _sb(1, I32), "ci": _sb(4, I32), "cf": _sb(4, F32), "c4": _sb(1, F32), "c0": _sb(1, F32), "mr": _sb(4, F32),
+    "m4": _sb(128, BF), "l16": _sb(NB, I32), "ulist": _sb(8, U16), "plist": _sb(HB, U16),
+    "k16": _sb(C, BF), "k4": _sb(4 * TW, BF), "mask16": _sb(H, BF), "keep16": _sb(H, BF), "gate16": _sb(C, BF),
+    "keep4": _sb(4 * TW, BF), "gate4": _sb(K, BF), "cq": _sb(H, F32), "gq": _sb(H, BF), "jv": _sb(C, BF),
+    "m1": _sb(C, F32), "sc": _sb(C, F32), "pex": _sb(C, F32), "pc": _sb(C, F32),
+    "junk": _sb(16 * HB * (HB - 1) + H, BF),
+    "rs": _sb(NB, F32), "gs": _sb(C, BF), "m2": _sb(C, F16), "sc2": _sb(C, F16), "nn": _sb(NB, F32), "pos": _sb(NB, F32),
+    "aoff": _sb(HB, U16), "moff": _sb(HB, U16), "sa": _sb(C + 8, F32), "fh": _sb(H, BF), "fl": _sb(H, BF), "nl": _sb(H, BF),
+    "nh": _sb(1, F32), "pl": _sb(H, F32),
+    "ft": _sb(520, BF), "fq": _sb(130, X4), "fs": _sb(130, U8), "d1": _sb(2 * NB + 1, F32), "nm": _sb(2 * NB + 1, F32),
     "dst": _sb(NB, F32), "doff": _sb(NB, U16),
-    "win0": _sb(C + K, BF), "win1": _sb(C + K, BF),
+    "win0": _sb(LOW + K, BF), "win1": _sb(LOW + K, BF),
     "bsn": _sb(K, BF), "boff": _sb(NB, U16), "bt": _sb(512, BF),
     "bq0": _sb(128, X4), "bs0": _sb(128, U8), "bq1": _sb(128, X4), "bs1": _sb(128, U8),
-    "lq": _sb(2 * K + 128, X4), "ls": _sb(2 * K + 128, U8), "ll": _sb(K, BF),
-    "hole": _sb(C, BF), "hs": _sb(C, BF), "ee": _sb(C, BF), "em": _sb(C, BF), "esn": _sb(C, BF), "toff": _sb(K + 2, U16),
-    "tt": _sb(4 * C + 16, BF), "tq": _sb(C, X4), "ts": _sb(C, U8), "rq": _sb(C, X4), "rsc": _sb(C, U8),
-    "om": _sb(C, BF), "osn": _sb(C, BF), "ooff": _sb(NB, U16), "ow": _sb(C + K, F32), "ob": _sb(C, F32),
+    "lq": _sb(2 * K + 128, X4), "ls": _sb(2 * K + 128, U8), "ll": _sb(K + 16, BF),
+    "hole": _sb(C, BF), "hs": _sb(C, BF), "ee": _sb(C + 4, BF), "em": _sb(C + 4 * TW + 4, BF), "esn": _sb(8 * TW, BF),
+    "toff": _sb(2 * TW + 2, U16),
+    "tt": _sb(32 * TW, BF), "tq": _sb(2 * (H + 2), X4), "ts": _sb(2 * (H + 2), U8),
+    "osn": _sb(C, BF), "ooff": _sb(NB, U16), "ow": _sb(C, F32), "og": _sb(C, F32), "ob": _sb(C, F32),
     "yb": _sb(C, F32),
 }
-for _i, (_n, _p) in enumerate(TILES):
-    SCRATCH["f%d" % _i] = _sb(4 * _n, BF)
-    SCRATCH["fq%d" % _i] = _sb(_n, X4)
-    SCRATCH["fs%d" % _i] = _sb(_n, U8)
+for _h in range(2):
+    for _i in range(2):
+        SCRATCH["f%d%d" % (_h, _i)] = _sb(4 * H, BF)
+    SCRATCH["fq%d" % _h] = _sb(H + 64 * _h, X4)
+    SCRATCH["fs%d" % _h] = _sb(H + 64 * _h, U8)
 for _i in range(8):
     SCRATCH["ps%d" % _i] = ("psum", [128, 512], F32)
 
@@ -61,13 +71,8 @@ def rank_program(g, core, T, topo):
     A, AF = AluOpType, ActivationFunctionType
     n = len(T.cores)
     nxt, prv = T.cores[(rank + 1) % n], T.cores[(rank - 1) % n]
-
-    def lanes(src, dst):
-        e = topo.engines(src, dst)
-        return e[::max(1, len(e) // 8)]
-
-    out_e, in_e = lanes(core, nxt), lanes(prv, core)
-    out_mask = sum(1 << e for e in out_e)
+    out_e, in_e = topo.engines(core, nxt), topo.engines(prv, core)
+    out_mask = topo.mask(core, nxt)
     rid, pid = topo.addr(nxt)[:2]
 
     Q = {"V": g.vector, "S": g.scalar, "P": g.tensor, "G": g, "Y": g.sync}
@@ -171,8 +176,8 @@ def rank_program(g, core, T, topo):
         else:
             op("G", lambda: g.iota(out, pattern, base, mult), (), w)
 
-    def asel(out, in_, pattern, cmp, base, mult, r, w):
-        op("G", lambda: g.affine_select(out, in_, pattern, cmp, 0.0, base, mult), r, w)
+    def asel(out, in_, pattern, cmp, base, mult, r, w, other=0.0):
+        op("G", lambda: g.affine_select(out, in_, pattern, cmp, other, base, mult), r, w)
 
     def four(name):
         return ["%s.%d" % (name, t) for t in range(4)]
@@ -181,10 +186,10 @@ def rank_program(g, core, T, topo):
     XC = [T.xc0, T.xc1, T.xc2]
 
     def xk(t, h):
-        return ["x%d.%d.%d" % (t, h, b) for b in range(4)]
+        return ["x%d.%d.%d" % (t, h, b) for b in range(8)]
 
     dma("Y", T.ub[:], T.u[:], "ldu", 16, w=["ub"])
-    dma("S", T.xc0[:, 0:4 * H], T.x[:, 0:4 * H], "ldx0", 16, w=xk(0, 0))
+    dma("Y", T.xc0[:, 0:4 * H], T.x[:, 0:4 * H], "ldx0", 16, w=xk(0, 0))
     dma("Y", T.xc0[:, 4 * H:4 * C], T.x[:, 4 * H:4 * C], "ldx1", 16, w=xk(0, 1))
     order("Y", xk(0, 0) + xk(0, 1), ())
     g.sync.dma_start(T.wq[:].bitcast(dt.uint8), T.wc[:]).then_inc(T.sem.ldw, 16)
@@ -195,8 +200,8 @@ def rank_program(g, core, T, topo):
 
     iota(T.pi[:], [[0, 1]], 0, 1, ["pi"], small=False)
     iota(T.l16[:], [[16, NB]], 0, 0, ["l16"], small=False)
-    iota(T.k16[:], [[0, NB], [1, 16]], 0, 0, ["k16"])
     iota(T.m4[:], [[1, 8], [0, 16]], 0, 0, ["m4"])
+    iota(T.k16[:, 0:H], [[0, HB], [1, 16]], 0, 0, ["k16"])
     fill(T.zb[:], 0.0, ["zb"])
     ts(T.ci[:, 0:1], T.pi[:], 4, A.arith_shift_right, r=["pi"], w=["ci0"])
     ts(T.ci[:, 1:2], T.pi[:], 15, A.bitwise_and, r=["pi"], w=["ci1"])
@@ -204,152 +209,233 @@ def rank_program(g, core, T, topo):
     ts(T.ci[:, 3:4], T.pi[:], 3, A.bitwise_and, r=["pi"], w=["ci3"])
     vcopy(T.ulist[:], T.l16[:, 0:8], ["l16"], ["ulist"])
     vcopy(T.cf[:], T.ci[:], ["ci0", "ci1", "ci2", "ci3"], ["cf"])
-    ts(T.plist[:], T.l16[:], 15.0, A.add, r=["l16"], w=["plist"])
-    fill(T.rs[:, 0:1], 0.0, ["rs0"])
-    fill(T.ones[:], 1.0, ["ones"])
-    ts(T.c4[:], T.cf[:, 3:4], 4.0 * OFF, A.add, r=["cf"], w=["c4"])
-    ts(T.jc[:], T.l16[:], T.cf[:, 1:2], A.add, -float(K), A.add, r=["l16", "cf"], w=["jc"])
-    fill(T.unit[:], 0.0, ["unit"])
-    ts(T.mask16[:], T.k16[:], T.cf[:, 1:2], A.is_equal, r=["k16", "cf"], w=["mask16"])
+    ts(T.plist[:], T.l16[:, 0:HB], 15.0, A.add, r=["l16"], w=["plist"])
     ts(T.onb[:, 0:512:4], T.m4[:], T.cf[:, 0:1], A.is_equal, r=["m4", "cf"], w=["onb.0"])
-    fill(T.win0[:], HOLE, ["win0"])
+    ts(T.onu[:], T.m4[:], T.cf[:, 0:1], A.is_equal, U, A.mult, r=["m4", "cf"], w=["onu"])
+    fill(T.rs[:], 0.0, ["rs%d" % p for p in range(NB)])
+    ts(T.mask16[:], T.k16[:, 0:H], T.cf[:, 1:2], A.is_equal, r=["k16", "cf"], w=["mask16"])
+    ts(T.c0[:], T.cf[:, 1:2], -1023.0, A.mult, r=["cf"], w=["c0"])
+    quant(T.fq1[:, 128:256], T.fs1[:, 128:256], T.zb[:, 0:512], ["zb"], ["qf1"])
 
-    def zero(i):
-        cols, planes = TILES[i]
-        a = 4 * 16 * min(p for p in planes if not isinstance(p, str)) if len(planes) == 4 else 0
-        act(T["f%d" % i][:, a:4 * cols], T.zb[:, 0:4 * cols - a], AF.Copy, ["zb"], four("f%d" % i))
+    def sfill(out, width, val, w):
+        if val:
+            act(out, T.zb[:, 0:width], AF.Identity, ["zb"], w, bias=val)
+        else:
+            act(out, T.zb[:, 0:width], AF.Copy, ["zb"], w)
 
-    zero(4)
-    zero(6)
-    zero(3)
-    act(T.keep16[:], T.k16[:], AF.Sign, ["k16"], ["keep16"])
+    def slot(p):
+        if p == 0 or p > 8:
+            return 0, 0, (12 - p) % 12
+        return 1, (128 if p < 5 else 0), (8 - p) % 4
+
+    def fkeys(h, i):
+        return ["f%d.%d" % (h, p) for p in range(HB) if slot(p)[0] == i]
+
+    def zero(h, i):
+        a = 4 * (80 if i else 144)
+        sfill(T["f%d%d" % (h, i)][:, a:4 * H], 4 * H - a, 0.0, fkeys(h, i))
+
+    zero(0, 1)
+    zero(0, 0)
     for t in (1, 2, 3):
         act(T.onb[:, t:512:4], T.onb[:, 0:512:4], AF.Copy, ["onb.0"], ["onb.%d" % t])
+    for t in (1, 2, 3):
+        act(T.dtb[:, t:512:4], T.onb[:, 0:512:4], AF.Copy, ["onb.0"], ["dtb.%d" % t])
     asel(T.dtb[:, 0:512:4], T.onb[:, 0:512:4], [[1, 128]], A.is_gt, 0, -1, ["onb.0"], ["dtb.0"])
-    asel(T.dtb[:, 1:512:4], T.onb[:, 0:512:4], [[-1, 128]], A.is_gt, 0, 1, ["onb.0"], ["dtb.1"])
-    asel(T.unit[:, 3:515:4], T.ones[:], [[-1, 128]], A.is_equal, 0, 1, ["ones"], ["unit"])
-    iota(T.k4[:], [[0, K], [1, 4]], 0, 0, ["k4"])
-    iota(T.cab[:], [[C - 2 * K + 1, 2], [-16, NB]], K - 1, 0, ["cab"])
+    iota(T.cq[:], [[-16, HB], [1024, 16]], H - 16, 0, ["cq"])
+    asel(T.sa[:, 0:K + 1], T.zb[:, 0:K + 1], [[0, K + 1]], A.is_gt, -1, 0, ["zb"], ["sa0"], -BIG)
+    asel(T.sa[:, K + H + 1:], T.zb[:, 0:K + 7], [[0, K + 7]], A.is_gt, -1, 0, ["zb"], ["sa"], BIG)
+    for s, (sg, cmp) in enumerate(((1, A.is_ge), (1, A.is_gt), (-1, A.is_gt), (-1, A.is_ge))):
+        asel(T.tri[:, s:512:4], T.onu[:], [[sg, 128]], cmp, 0, -sg, ["onu"], ["tri.%d" % s])
     iota(T.jv[:], [[1, C]], -OFF, 0, ["jv"])
-    iota(T.ow[:, 0:C], [[1, C]], 0, 0, ["ow0"])
+    iota(T.k4[:], [[0, TW], [1, 4]], 0, 0, ["k4"])
+    iota(T.k16[:, H:C], [[0, HB], [1, 16]], 0, 0, ["k16b"])
     quant(T.uq[:], T.us[:], T.ub[:], ["ub"], ["uq"])
     act(T.ups[:], T.us[:].indirect(T.ulist[:]), AF.Copy, ["uq", "ulist"], ["ups"])
     vcopy(T.upq[:].bitcast(dt.uint32), T.uq[:].bitcast(dt.uint32).indirect(T.ulist[:]), ["uq", "ulist"], ["upq"])
-    zero(5)
-    for t in (2, 3):
-        act(T.dtb[:, t:512:4], T.onb[:, 0:512:4], AF.Copy, ["onb.0"], ["dtb.%d" % t])
-    for i in (0, 1, 2):
-        zero(i)
+    act(T.keep16[:], T.k16[:, 0:H], AF.Sign, ["k16"], ["keep16"])
+    zero(1, 1)
+    zero(1, 0)
+    act(T.gq[:], T.cq[:], AF.Abs, ["cq", "c0"], ["gq"], bias=T.c0[:])
+
+    def unit(b):
+        quant(T.eq[:, 128 * b:128 * b + 128], T.es[:, 128 * b:128 * b + 128], T.unit[:, 3 - b:515 - b], ["unit"], ["eq%d" % b])
 
     def quant_state(t, h):
         quant(T.xq[:, h * H:h * H + H], T.xs[:, h * H:h * H + H], XC[t][:, 4 * h * H:4 * h * H + 4 * H], xk(t, h), ["xq%d" % h])
 
-    def scores(bank, cols):
-        mm(PS[bank][:, 0:cols], T.upq[:], T.ups[:], T.xq[:, 0:cols], T.xs[:, 0:cols], True, True,
-           ["upq", "ups", "xq0"] + (["xq1"] if cols > H else []), ["ps%d" % bank])
+    def scores(h, which=(0, 1)):
+        for bank in [4 * h + i for i in which]:
+            mm(PS[bank][:, 0:H], T.upq[:], T.ups[:], T.xq[:, h * H:h * H + H], T.xs[:, h * H:h * H + H], True, True,
+               ["upq", "ups", "xq%d" % h], ["ps%d" % bank])
+
+    def masked(h):
+        tt(T.m1[:, h * H:h * H + H], PS[4 * h][:, 0:H], T.mask16[:], A.mult, ["ps%d" % (4 * h), "mask16"], ["m1%d" % h])
 
     def pivots(h):
-        a = h * H
-        tt(T.m1[:, a:a + H], PS[h][:, a:a + H], T.mask16[:, a:a + H], A.mult, ["ps%d" % h, "mask16"], ["m1%d" % h])
-        return lambda: scan(T.sc[:, a:a + H], T.keep16[:, a:a + H], T.m1[:, a:a + H], 0.0, A.mult, A.add, ["keep16", "m1%d" % h], ["sc%d" % h])
+        scan(T.sc[:, h * H:h * H + H], T.keep16[:], T.m1[:, h * H:h * H + H], 0.0, A.mult, A.add, ["keep16", "m1%d" % h], ["sc%d" % h])
 
-    def plane(p):
-        i, s = [(i, pl.index(p)) for i, (c, pl) in enumerate(TILES) if p in pl][0]
-        F, key = T["f%d" % i], "f%d.%d" % (i, s)
-        if isinstance(p, str):
-            tt(F[:, s:4 * C:4], T.pex[:], PS[1][:, 0:C], A.is_lt if p == "a" else A.is_le, ["pex", "ps1"], [key])
+    def keep_scores(h):
+        act(T.pc[:, h * H:h * H + H], PS[4 * h + 1][:, 0:H], AF.Copy, ["ps%d" % (4 * h + 1)], ["pc%d" % h])
+
+    def spread(h):
+        act(T.pex[:, h * H:h * H + H], T.sc[:, h * H:h * H + H].indirect(T.plist[:]), AF.Copy, ["sc%d" % h, "plist"], ["pex%d" % h])
+
+    def view(h, p):
+        i, a, s = slot(p)
+        return T["f%d%d" % (h, i)][:, 4 * a + s:4 * (a + (16 * p or H)):4]
+
+    def plane(t, h, p):
+        key, c = "f%d.%d" % (h, p), h * HB + p
+        piv = T.sc[:, 16 * c + 15:16 * c + 16]
+        a = 8 * (h * HB * (HB - 1) + p * (p - 1))
+        junk = T.junk[:, a:a + 16 * p]
+        if p == 0:
+            tt(view(h, 0), T.pex[:, h * H:h * H + H], PS[4 * h][:, 0:H], A.is_ge, ["pex%d" % h, "ps%d" % (4 * h)], [key])
+        elif p in ON_S[t][h]:
+            act(junk, T.pc[:, h * H:h * H + 16 * p], AF.Sign, ["pc%d" % h, "sc%d" % h], ["j%d" % c], scale=-1.0, bias=piv)
         else:
-            h = 16 * p // H
-            ts(F[:, s:64 * p:4], PS[h][:, 0:16 * p], T.sc[:, 16 * p + 15:16 * p + 16], A.is_ge, r=["ps%d" % h, "sc%d" % h], w=[key])
-            a = 8 * p * (p - 1)
-            act(T.junk[:, a:a + 16 * p], F[:, s:64 * p:4], AF.Copy, [key], ["rs%d" % p], accum_out=T.rs[:, p:p + 1])
+            ts(view(h, p), PS[4 * h][:, 0:16 * p], piv, A.is_lt, r=["ps%d" % (4 * h), "sc%d" % h], w=[key])
 
-    def pack(i):
-        quant(T["fq%d" % i][:], T["fs%d" % i][:], T["f%d" % i][:], four("f%d" % i), ["qf%d" % i])
+    def rows(t, h, p):
+        key, c = "f%d.%d" % (h, p), h * HB + p
+        a = 8 * (h * HB * (HB - 1) + p * (p - 1))
+        junk = T.junk[:, a:a + 16 * p]
+        if p in ON_S[t][h]:
+            act(view(h, p), junk, AF.Relu, ["j%d" % c], [key, "rs%d" % c], accum_out=T.rs[:, c:c + 1])
+        else:
+            act(junk, view(h, p), AF.Copy, [key], ["rs%d" % c, "j%d" % c], accum_out=T.rs[:, c:c + 1])
 
-    def columns(i):
-        sq, ss, sk = (T.dtq, T.dts, "dtq") if i == 0 else (T.onq, T.ons, "onq")
-        mm(PS[2][:, 0:TILES[i][0]], sq[:], ss[:], T["fq%d" % i][:], T["fs%d" % i][:], i == 0, i == 3, [sk, "qf%d" % i], ["ps2"])
+    def pack(h, i):
+        quant(T["fq%d" % i][:, 0:H], T["fs%d" % i][:, 0:H], T["f%d%d" % (h, i)][:], fkeys(h, i), ["qf%d" % i])
+
+    def columns(h):
+        bank = "ps%d" % (4 * h + 2)
+        mm(PS[4 * h + 2][:, 0:H], T.dtq[:], T.dts[:], T.fq0[:], T.fs0[:], True, False, ["dtq", "qf0"], [bank])
+        for a in (0, 128):
+            mm(PS[4 * h + 2][:, 0:128], T.onq[:], T.ons[:], T.fq1[:, a:a + 128], T.fs1[:, a:a + 128], False, a > 0, ["onq", "qf1"], [bank])
+
+    def inside(h):
+        scan(T.gs[:, h * H:h * H + H], T.gq[:], view(h, 0), 512.0, A.min, A.add, ["gq", "f%d.0" % h], ["gs%d" % h])
+
+    def col_masked(h):
+        tt(T.m2[:, h * H:h * H + H], PS[4 * h + 2][:, 0:H], T.mask16[:], A.mult, ["ps%d" % (4 * h + 2), "mask16"], ["m2%d" % h])
+
+    def col_list(h):
+        scan(T.sc2[:, h * H:h * H + H], T.keep16[:], T.m2[:, h * H:h * H + H], 0.0, A.mult, A.add, ["keep16", "m2%d" % h], ["sc2%d" % h])
+
+    def row_list(h):
+        tt(T.nn[:, h * HB:h * HB + HB], T.gs[:, h * H + 15:h * H + H:16], T.rs[:, h * HB:h * HB + HB], A.add,
+           ["gs%d" % h] + ["rs%d" % (h * HB + p) for p in range(HB)], ["nn%d" % h])
 
     quant_state(0, 0)
-    scores(0, H)
-    quant_state(0, 1)
-    scores(1, C)
+    scores(0)
+    quant(T.onq[:], T.ons[:], T.onb[:], four("onb"), ["onq"])
+    quant(T.dtq[:], T.dts[:], T.dtb[:], four("dtb"), ["dtq"])
 
     for t in range(R):
         last = t == R - 1
         X, win, wk = XC[t], T["win%d" % t], "win%d" % t
         xall = xk(t, 0) + xk(t, 1)
-        rest = pivots(0)
+        masked(0)
         if t == 0:
-            quant(T.onq[:], T.ons[:], T.onb[:], four("onb"), ["onq"])
-        rest()
-        for p in (9, 8, 7, 6):
-            plane(p)
-        if t > 0:
-            quant_state(t, 1)
-            scores(1, C)
-        pack(4)
-        for p in (11, 10, 5, 4, 3, 2):
-            plane(p)
-        rest = pivots(1)
-        pack(6)
-        rest()
-        plane(1)
-        act(T.pex[:], T.sc[:].indirect(T.plist[:]), AF.Copy, ["sc0", "sc1", "plist"], ["pex"])
-        for p in (23, 22, 21, 20, 19, 18, "a", "b"):
-            plane(p)
+            quant_state(0, 1)
+            scores(1)
+        pivots(0)
+        if ON_S[t][0]:
+            keep_scores(0)
+        spread(0)
+        for p in ON_S[t][0]:
+            plane(t, 0, p)
+        for p in range(HB - 1, 0, -1):
+            if p not in ON_S[t][0]:
+                plane(t, 0, p)
+            rows(t, 0, p)
+            if t > 0 and p == 8:
+                quant_state(t, 1)
+                scores(1)
+        masked(1)
+        plane(t, 0, 0)
+        pivots(1)
+        pack(0, 0)
+        pack(0, 1)
+        columns(0)
+        keep_scores(1)
+        spread(1)
+        for p in ON_S[t][1]:
+            plane(t, 1, p)
+        for p in ON_S[t][1]:
+            rows(t, 1, p)
+        if not ON_S[t][0]:
+            keep_scores(0)
+        inside(0)
+        mine = [p for p in range(HB - 1, 0, -1) if p not in ON_S[t][1]]
+        for p in mine[:2]:
+            plane(t, 1, p)
+        col_masked(0)
+        plane(t, 1, mine[2])
+        col_list(0)
+        row_list(0)
+        for p in mine[3:]:
+            plane(t, 1, p)
+        for p in mine:
+            rows(t, 1, p)
+        posA, negB = T.pos[:, 0:HB], T.pos[:, HB:NB]
+        tt(posA, T.nn[:, 0:HB], T.sc2[:, 15:H:16], A.subtract, ["nn0", "sc20"], ["posA"])
+        plane(t, 1, 0)
+        vcopy(T.aoff[:], posA, ["posA"], ["aoff"])
+        pack(1, 1)
+        pack(1, 0)
+        columns(1)
+        inside(1)
+        vcopy(T.sa[:, K:K + H + 8].indirect(T.aoff[:]), T.pc[:, 0:H], ["pc0", "aoff"], ["sa", "sa0"])
         if t == 0:
-            quant(T.dtq[:], T.dts[:], T.dtb[:], four("dtb"), ["dtq"])
-        pack(5)
-        pack(0)
-        for p in (17, 16, 15, 14):
-            plane(p)
-        pack(1)
-        for i in (0, 4, 6, 5, 1):
-            columns(i)
-        for p in (13, 12):
-            plane(p)
-        pack(2)
-        columns(2)
-        pack(3)
-        columns(3)
+            sfill(T.tri[:, 512:520], 8, 0.0, ["tri.z"])
+            sfill(T.ft[:], 520, 0.0, ["lo0", "lo1", "lp0", "lp1", "hi0", "hi1"])
+        col_masked(1)
+        row_list(1)
+        col_list(1)
+        tt(negB, T.sc2[:, H + 15:C:16], T.nn[:, HB:NB], A.subtract, ["nn1", "sc21"], ["negB"])
         if t == 0:
-            act(T.ft[:], T.zb[:], AF.Copy, ["zb"], ["ft.lo", "ft.hl"])
+            quant(T.s1q[:], T.s1s[:], T.tri[:, 0:512], four("tri"), ["s1q"])
+        ts(T.moff[:], negB, float(H + 1), A.add, r=["negB"], w=["moff"])
+        act(T.pl[:], T.sa[:, 0:H + 8].indirect(T.moff[:]), AF.Copy, ["sa", "moff"], ["pl"])
+        tt(T.fh[:], T.sa[:, H:].indirect(T.moff[:]), T.pc[:, H:C], A.is_lt, ["sa", "moff", "pc1"], ["fh"])
+        act(T.junk[:, 16 * HB * (HB - 1):], T.fh[:], AF.Copy, ["fh"], ["nh"], accum_out=T.nh[:])
+        tt(T.fl[:], T.pl[:], PS[4][:, 0:H], A.is_lt, ["pl", "ps4"], ["fl"])
+        if t == 0:
+            quant(T.s2q[:], T.s2s[:], T.tri[:, 2:514], four("tri") + ["tri.z"], ["s2q"])
+            sfill(T.d1[:, NB + 1:], NB, 0.0, ["d1z"])
+            sfill(win[:], LOW + K, HOLE, [wk])
+            sfill(T.unit[:], 520, 0.0, ["unit"])
+            asel(T.unit[:, 3:515:4], T.onb[:, 0:512:4], [[-1, 128]], A.is_equal, 0, 1, ["onb.0"], ["unit"])
+            sfill(T.bt[:, C:512], 512 - C, 0.0, ["bt.z"])
+        scan(T.nl[:], T.fl[:], T.zb[:, 0:H], 0.0, A.add, A.add, ["fl", "zb"], ["nl"])
+        nh, nl = T.nh[:], T.nl[:, H - 1:H]
+        o = 16 + 8 * NB
+        ts(T.ft[:, o + 1:o + 8 * HB:8], posA, nh, A.subtract, float(K), A.is_gt, r=["posA", "nh"], w=["hi0"])
+        ts(T.ft[:, o + 1 + 8 * HB:o + 8 * NB:8], negB, nh, A.subtract, -float(H), A.is_lt, r=["negB", "nh"], w=["hi1"])
+        for a, key, ca, cb in ((8, "lo", A.is_le, A.is_ge), (o, "lp", A.is_gt, A.is_lt)):
+            ts(T.ft[:, a:a + 8 * HB:8], posA, nl, A.subtract, -float(K), ca, r=["posA", "nl"], w=[key + "0"])
+            ts(T.ft[:, a + 8 * HB:a + 8 * NB:8], negB, nl, A.subtract, -float(H), cb, r=["negB", "nl"], w=[key + "1"])
+        quant(T.fq[:], T.fs[:], T.ft[:], ["lo0", "lo1", "lp0", "lp1", "hi0", "hi1"], ["fq"])
+        mm(PS[3][:, 0:128], T.s1q[:], T.s1s[:], T.fq[:, 2:130], T.fs[:, 2:130], True, False, ["s1q", "fq"], ["ps3"])
+        mm(PS[3][:, 0:128], T.s2q[:], T.s2s[:], T.fq[:, 0:128], T.fs[:, 0:128], False, True, ["s2q", "fq"], ["ps3"])
+        tt(T.d1[:, 0:NB + 1], T.ft[:, 8:o:8], T.ft[:, 0:o - 8:8], A.subtract, ["lo0", "lo1"], ["d1"])
+        if t == 0:
+            ts(T.gate4[:], T.k4[:, 0:K], T.cf[:, 2:3], A.is_equal, 2000.0, A.mult, r=["k4", "cf"], w=["gate4"])
+            act(T.gate4[:], T.gate4[:], AF.Identity, ["gate4"], ["gate4"], bias=-1000.0)
             act(T.keep4[:], T.k4[:], AF.Sign, ["k4"], ["keep4"])
-            act(T.bt[:, C:512], T.zb[:, 0:512 - C], AF.Copy, ["zb"], ["bt.z"])
-            ts(T.mask4[:], T.k4[:], T.cf[:, 2:3], A.is_equal, r=["k4", "cf"], w=["mask4"])
-        else:
-            fill(win[:], HOLE, [wk])
-        tt(T.m2[:], PS[2][:, 0:C], T.mask16[:], A.mult, ["ps2", "mask16"], ["m2"])
-        rsk = ["rs%d" % p for p in range(NB)]
-        tt(T.ab[:, 0:NB], T.rs[:], T.cab[:, 0:NB], A.add, rsk + ["cab"], ["ab0"])
-        scan(T.sc2[:], T.keep16[:], T.m2[:], 0.0, A.mult, A.add, ["keep16", "m2"], ["sc2"])
-        tt(T.ab[:, NB:2 * NB], T.rs[:], T.cab[:, NB:2 * NB], A.add, rsk + ["cab"], ["ab1"])
-        cs = T.sc2[:, 15:C:16]
-        lo = T.ft[:, 1:4 * NB:4]
-        tt(T.hi[:], T.ab[:, NB:2 * NB], cs, A.is_le, ["ab1", "sc2"], ["hi"])
-        tt(lo, T.ab[:, 0:NB], cs, A.is_ge, ["ab0", "sc2"], ["ft.lo"])
-        tt(T.ft[:, 4 * NB + 1:8 * NB:4], T.hi[:], lo, A.subtract, ["hi", "ft.lo"], ["ft.hl"])
-        quant(T.fq[:], T.fs[:], T.ft[:], ["ft.lo", "ft.hl"], ["fq"])
-        mm(PS[3][:, 0:128], T.onq[:], T.ons[:], T.fq[:], T.fs[:], True, True, ["onq", "fq"], ["ps3"])
-        mm(PS[0][:, 0:128], T.dtq[:], T.dts[:], T.fq[:], T.fs[:], True, True, ["dtq", "fq"], ["ps0"])
-        ts(T.pre[:, 0:NB], lo, 1000.0, A.mult, C - 1 - 1000.0, A.add, r=["ft.lo"], w=["pre0"])
-        tt(T.pre[:, NB:2 * NB], T.jc[:], T.hi[:], A.subtract, ["jc", "hi"], ["pre1"])
-        if t == 0:
-            ts(T.gate4[:], T.mask4[:, 0:K], 2000.0, A.mult, -1000.0, A.add, r=["mask4"], w=["gate4"])
-        else:
-            quant(T.vq[:], T.vs[:], T.vb[:], ["vb"], ["vq"])
-        scan(T.inc[:], PS[3][:, 0:2 * NB], T.zb[:, 0:2 * NB], 0.0, A.add, A.add, ["ps3", "zb"], ["inc"])
-        tt(T.x1[:], T.pre[:], PS[0][:, 0:2 * NB], A.subtract, ["pre0", "pre1", "ps0"], ["x1"])
-        tt(T.nm[:], T.x1[:], T.inc[:], A.add, ["x1", "inc"], ["nm"])
-        tt(T.dst[:], T.nm[:, 0:NB], T.nm[:, NB:2 * NB], A.max, ["nm"], ["dst"])
-        vcopy(T.doff[:], T.dst[:], ["dst"], ["doff"])
+            ts(T.c4[:], T.cf[:, 3:4], 4.0 * OFF, A.add, r=["cf"], w=["c4"])
+            ts(T.mr[:], T.k4[:, 0:4], T.cf[:, 2:3], A.is_equal, r=["k4", "cf"], w=["mr"])
+        scan(T.nm[:], PS[3][:, 0:4 * NB + 2:2], T.d1[:], (LOW - 1 - 512) * U, A.add, A.add, ["ps3", "d1", "d1z"], ["nm"])
+        tt(T.dst[:], T.nm[:, 0:NB], T.nm[:, NB + 1:2 * NB + 1], A.max, ["nm"], ["dst"])
+        ts(T.doff[:], T.dst[:], 512.0, A.mult, r=["dst"], w=["doff"])
         vcopy(win[:].indirect(T.doff[:]), T.jv[:], ["jv", "doff"], [wk])
         if last:
-            send(T.ll[:], win[:, C:C + K], "arrl", [wk])
+            send(T.ll[:, 16:16 + K], win[:, LOW:LOW + K], "arrl", [wk])
             arrival("ll", "arrl", 1)
-        scan(T.bsn[:], T.gate4[:], win[:, C:C + K], 0.0, A.max, A.min, ["gate4", wk], ["bsn"])
+        scan(T.bsn[:], T.gate4[:], win[:, LOW:LOW + K], 0.0, A.max, A.min, ["gate4", wk], ["bsn"])
         ts(T.boff[:], T.bsn[:, 3:K:4], 4.0, A.mult, T.c4[:], A.add, r=["bsn", "c4"], w=["boff"])
         act(T.bt[:, 2 * K:4 * K], X[:, 0:4 * C].indirect(T.boff[:, NB // 2:NB]), AF.Copy, xall + ["boff"], ["bt.1"])
         vcopy(T.bt[:, 0:2 * K], X[:, 0:4 * C].indirect(T.boff[:, 0:NB // 2]), xall + ["boff"], ["bt.0"])
@@ -359,96 +445,125 @@ def rank_program(g, core, T, topo):
         send(T.lq[:, land:land + K].bitcast(dt.uint8), bq[:, 0:K].bitcast(dt.uint8), "arr%d" % t, ["bq%d" % t])
         send(T.ls[:, land:land + K], bs[:, 0:K], "arr%d" % t, ["bq%d" % t])
         arrival("land%d" % t, "arr%d" % t, 2)
-        if t == 0:
-            quant(T.lq[:, K:K + 128], T.ls[:, K:K + 128], T.zb[:], ["zb"], ["lfill"])
-            for b in range(4):
-                quant(T.eq[:, 128 * b:128 * b + 128], T.es[:, 128 * b:128 * b + 128], T.unit[:, 3 - b:515 - b], ["unit"], ["eq%d" % b])
-        ts(T.hole[:], win[:, 0:C], 200.0, A.is_gt, r=[wk], w=["hole"])
-        scan(T.hs[:], T.hole[:], T.zb[:, 0:C], float(C - 1 - OFF), A.add, A.add, ["hole", "zb"], ["hs"])
-        tt(T.ee[:], win[:, 0:C], T.hs[:], A.min, [wk, "hs"], ["ee"])
-        tt(T.em[:], T.ee[:], T.mask4[:], A.mult, ["ee", "mask4"], ["em"])
-        scan(T.esn[:], T.keep4[:], T.em[:], 0.0, A.mult, A.add, ["keep4", "em"], ["esn"])
-        ts(T.toff[:, 0:K], T.esn[:, 3:C:4], 4.0, A.mult, T.c4[:], A.add, r=["esn", "c4"], w=["toff0"])
-        ts(T.toff[:, K:K + 1], T.esn[:, 3:4], 4.0, A.mult, T.c4[:], A.add, r=["esn", "c4"], w=["toff1"])
         if last:
-            act(T.ow[:, C:C + K], T.ll[:], AF.Identity, ["ll"], ["ow1"], bias=float(C + OFF))
-        view, first = (0, 0) if t == 0 else (land + K - 128, 128 - K)
+            act(T.ow[:], win[:, 0:C], AF.Identity, [wk], ["ow"], bias=float(OFF))
+        else:
+            sfill(T.win1[:], LOW + K, HOLE, ["win1"])
+            sfill(T.ll[:, 0:16], 16, -float(OFF), ["ll0"])
+        ts(T.hole[:], win[:, 0:C], 200.0, A.is_gt, r=[wk], w=["hole"])
+        if t == 0:
+            quant(T.lq[:, K:K + 128], T.ls[:, K:K + 128], T.zb[:, 0:512], ["zb"], ["lfill"])
+        scan(T.hs[:], T.hole[:], T.zb[:, 0:C], float(C - 1 - OFF), A.add, A.add, ["hole", "zb"], ["hs"])
+        if t == 0:
+            unit(0)
+        scan(T.ee[:, 0:C], T.hs[:], win[:, 0:C], -1000.0, A.max, A.min, [wk, "hs"], ["ee"])
+        if t == 0:
+            unit(1)
+        else:
+            scan(T.osn[:], T.gate16[:], T.hs[:], 0.0, A.max, A.min, ["gate16", "hs"], ["osn"])
+        vcopy(T.ee[:, C:C + 4], T.ee[:, 0:4], ["ee"], ["ee2"])
+        if t == 0:
+            unit(2)
+        else:
+            ts(T.ooff[:], T.osn[:, 15:C:16], float(OFF + 16 - C), A.add, r=["osn"], w=["ooff"])
+        wide = C // 4 + TW + 1
+        for r4 in range(4):
+            a = K * (r4 % 2) + r4 // 2
+            o_, i_ = T.em[:, r4:4 * wide:4], T.ee[:, a:a + 2 * wide - 1:2]
+            if r4 < 2:
+                ts(o_, i_, T.mr[:, r4:r4 + 1], A.mult, r=["ee", "ee2", "mr"], w=["em.%d" % r4])
+            else:
+                act(o_, i_, AF.Copy, ["ee", "ee2", "mr"], ["em.%d" % r4], scale=T.mr[:, r4:r4 + 1])
+        if t == 0:
+            unit(3)
+        else:
+            act(T.og[:], T.ll[:].indirect(T.ooff[:]), AF.Identity, ["ll", "ll0", "ooff"], ["og"], bias=float(C + OFF))
+        for h in range(2):
+            scan(T.esn[:, 4 * TW * h:4 * TW * (h + 1)], T.keep4[:], T.em[:, C * h:C * h + 4 * TW], 0.0, A.mult, A.add,
+                 ["keep4"] + four("em"), ["esn%d" % h])
+        for h in range(2):
+            ts(T.toff[:, (TW + 1) * h:(TW + 1) * h + TW], T.esn[:, 4 * TW * h + 3:4 * TW * (h + 1):4], 4.0, A.mult, T.c4[:], A.add,
+               r=["esn%d" % h, "c4"], w=["toff%d" % h])
+        at, first = (0, 0) if t == 0 else (land + K - 128, 128 - K)
         for b in range(4):
             mm(PS[4 + b][:, 0:128], T.eq[:, 128 * b:128 * b + 128], T.es[:, 128 * b:128 * b + 128],
-               T.lq[:, view:view + 128], T.ls[:, view:view + 128], True, True, ["eq%d" % b, "lfill", "land%d" % t], ["ps%d" % (4 + b)])
+               T.lq[:, at:at + 128], T.ls[:, at:at + 128], True, True, ["eq%d" % b, "lfill", "land%d" % t], ["ps%d" % (4 + b)])
         for b in range(4):
-            o, i_ = X[:, 4 * C + b:4 * (C + K):4], PS[4 + b][:, first:first + K]
-            if b < 3:
-                act(o, i_, AF.Copy, ["ps%d" % (4 + b)], ["came%d" % b])
+            o_, i_ = X[:, 4 * C + b:4 * (C + K):4], PS[4 + b][:, first:first + K]
+            if b % 2 == 0:
+                act(o_, i_, AF.Copy, ["ps%d" % (4 + b)], ["came%d" % b])
             else:
-                vcopy(o, i_, ["ps%d" % (4 + b)], ["came%d" % b])
-        src = xall + ["came%d" % b for b in range(4)] + ["toff0", "toff1"]
-        cut = [0, 24, 50, 66, K + 1]
+                vcopy(o_, i_, ["ps%d" % (4 + b)], ["came%d" % b])
+        src = xall + ["came%d" % b for b in range(4)]
 
-        def pick(e, k):
-            o, i_ = T.tt[:, 16 * cut[k]:16 * cut[k + 1]], X[:].indirect(T.toff[:, cut[k]:cut[k + 1]])
+        def pick(e, h, a, b):
+            o_ = T.tt[:, 16 * (TW * h + a):16 * (TW * h + b)]
+            i_ = X[:].indirect(T.toff[:, (TW + 1) * h + a:(TW + 1) * h + b])
             if e == "V":
-                vcopy(o, i_, src, ["tt%d" % k])
+                vcopy(o_, i_, src + ["toff%d" % h], ["tt%d%s" % (h, e)])
             else:
-                act(o, i_, AF.Copy, src, ["tt%d" % k])
+                act(o_, i_, AF.Copy, src + ["toff%d" % h], ["tt%d%s" % (h, e)])
 
-        def quant_t(h, keys):
-            a = h * H
-            quant(T.tq[:, a:a + H], T.ts[:, a:a + H], T.tt[:, 4 * a:4 * a + 4 * H], keys, ["tq%d" % h])
-            quant(T.rq[:, a:a + H], T.rsc[:, a:a + H], T.tt[:, 4 * a + 4:4 * a + 4 * H + 4], keys, ["rq%d" % h])
+        def quant_t(h):
+            a = h * (H + 2)
+            quant(T.tq[:, a:a + H + 2], T.ts[:, a:a + H + 2], T.tt[:, 16 * TW * h:16 * TW * h + 4 * (H + 2)], ["tt%dV" % h, "tt%dS" % h], ["tq%d" % h])
 
-        steps = ((0, 0), (0, 1), (1, 0), (1, 1), (0, 2), (1, 2), (0, 3), (1, 3))
-
-        def layer(h, part):
-            a = h * H
-            for z, b in part:
-                wq, ws, mq, ms, mk = (T.zq, T.zsc, T.rq, T.rsc, "rq%d" % h) if z else (T.wq, T.wsc, T.tq, T.ts, "tq%d" % h)
-                mm(PS[4 * h + b][:, 0:H], wq[:, 128 * b:128 * b + 128], ws[:, 128 * b:128 * b + 128],
-                   mq[:, a:a + H], ms[:, a:a + H], z == 0, z == 1, ["wz", mk], ["ps%d" % (4 * h + b)])
+        def layer(h, banks):
+            for b in banks:
+                for z in range(2):
+                    a = h * (H + 2) + 2 * z
+                    wq, ws = (T.zq, T.zsc) if z else (T.wq, T.wsc)
+                    mm(PS[4 * h + b][:, 0:H], wq[:, 128 * b:128 * b + 128], ws[:, 128 * b:128 * b + 128],
+                       T.tq[:, a:a + H], T.ts[:, a:a + H], z == 0, z == 1, ["wz", "tq%d" % h], ["ps%d" % (4 * h + b)])
 
         def new_state(e, h, b):
-            o, i_ = XC[t + 1][:, 4 * h * H + b:4 * h * H + 4 * H:4], PS[4 * h + b][:, 0:H]
-            r, w = ["ps%d" % (4 * h + b)], [xk(t + 1, h)[b]]
-            if e == "V":
-                ts(o, i_, 0.015625, A.mult, r=r, w=w)
-            else:
-                act(o, i_, AF.Copy, r, w, scale=0.015625)
+            for a in range(2):
+                c = 4 * (h * H + a * K)
+                o_, i_ = XC[t + 1][:, c + b:c + 4 * K:4], PS[4 * h + b][:, a:H:2]
+                r, w = ["ps%d" % (4 * h + b)], [xk(t + 1, h)[2 * b + a]]
+                if e == "V":
+                    ts(o_, i_, 0.015625, A.mult, r=r, w=w)
+                else:
+                    act(o_, i_, AF.Copy, r, w, scale=0.015625)
 
-        pick("S", 1)
-        pick("V", 0)
-        quant_t(0, ["tt0", "tt1"])
-        layer(0, steps)
-        pick("S", 3)
-        pick("V", 2)
-        quant_t(1, ["tt1", "tt2", "tt3"])
+        pick("S", 0, 26, TW)
+        pick("V", 0, 0, 26)
+        quant_t(0)
+        layer(0, range(4))
+        pick("S", 1, 26, TW)
+        pick("V", 1, 0, 26)
+        quant_t(1)
         new_state("S", 0, 0)
         new_state("V", 0, 1)
+        if t == 0:
+            quant(T.vq[:], T.vs[:], T.vb[:], ["vb"], ["vq"])
         new_state("S", 0, 2)
         new_state("V", 0, 3)
         quant_state(t + 1, 0)
-        layer(1, steps[:4])
+        layer(1, (0, 1))
         if not last:
-            scores(0, H)
-        layer(1, steps[4:])
+            scores(0, (0,))
+            ts(T.gate16[:], T.k16[:], T.cf[:, 1:2], A.is_equal, 2000.0, A.mult, r=["k16", "k16b", "cf"], w=["gate16"])
+        layer(1, (2, 3))
+        if not last:
+            scores(0, (1,))
+        else:
+            scan(T.ob[:], T.og[:], T.ow[:], 0.0, A.max, A.min, ["og", "ow"], ["ob"])
         for b in range(4):
-            new_state("S", 1, b)
+            new_state("V" if last and b == 3 else "S", 1, b)
 
     store("Y", T.oc[:, 0:4 * H], T.xq[:, 0:H].bitcast(dt.uint8), ["xq0"])
+    store("Y", T.ol[:], T.ob[0:128:16, :], ["ob"])
     mm(PS[0][:, 0:H], T.vq[:], T.vs[:], T.xq[:, 0:H], T.xs[:, 0:H], True, True, ["vq", "xq0"], ["ps0"])
-    tt(T.om[:], T.ee[:], T.mask16[:], A.mult, ["ee", "mask16"], ["om"])
-    scan(T.osn[:], T.keep16[:], T.om[:], 0.0, A.mult, A.add, ["keep16", "om"], ["osn"])
     quant_state(R, 1)
     mm(PS[1][:, 0:H], T.vq[:], T.vs[:], T.xq[:, H:C], T.xs[:, H:C], True, True, ["vq", "xq1"], ["ps1"])
     act(T.yb[:, 0:H], PS[0][:, 0:H], AF.Copy, ["ps0"], ["yb0"])
-    ts(T.ooff[:], T.osn[:, 15:C:16], float(OFF), A.add, r=["osn"], w=["ooff"])
-    store("Y", T.y[:, 0:H], T.yb[:, 0:H], ["yb0"])
+    store("S", T.y[:, 0:H], T.yb[:, 0:H], ["yb0"])
     store("Y", T.oc[:, 4 * H:4 * C], T.xq[:, H:C].bitcast(dt.uint8), ["xq1"])
     for k in range(4):
         store("Y", T.osc[4 * k:4 * k + 4, :], T.xs[32 * k:32 * k + 4, :], ["xq0", "xq1"])
-    act(T.yb[:, H:C], PS[1][:, 0:H], AF.Copy, ["ps1"], ["yb1"])
-    vcopy(T.ob[:], T.ow[:].indirect(T.ooff[:]), ["ow0", "ow1", "ooff"], ["ob"])
+    vcopy(T.yb[:, H:C], PS[1][:, 0:H], ["ps1"], ["yb1"])
     store("S", T.y[:, H:C], T.yb[:, H:C], ["yb1"])
-    store("Y", T.ol[:], T.ob[0:128:16, :], ["ob"])
 
     for e in ("V", "S", "P", "G"):
         g.wait_ge(T.sem["s" + e], cnt[e])

@@ -9,10 +9,27 @@ HOLE = 1024.0
 BIG = 9.0e29
 U = 1.0 / 512
 LOW = 512 - K
-TW = 49
-ON_S = (((), (11, 10)), ((), (11, 10)))
+TW = 50
+G = 131072.0
+ON_S = (((11, 10), (11, 10, 9)), ((11,), (11, 10, 9)))
 
-BF, F32, F16, I32, U16, U8, X4 = "bfloat16", "float32", "float16", "int32", "uint16", "uint8", "float8_e4m3fn_x4"
+BF, F32, I32, U16, U8, X4 = "bfloat16", "float32", "int32", "uint16", "uint8", "float8_e4m3fn_x4"
+
+ORDER = [int(_x) for _x in """
+0 1 2 3 4 7 5 10 12 13 11 6 8 14 18 15 40 16 42 9 53 44 19 45 49 50 41 24 20 21 58 43 25 52 47 54 57 17 55 60 59 61 29 30 37
+34 35 38 36 32 33 31 39 88 51 62 26 27 64 48 63 80 68 84 78 46 28 65 66 79 70 82 67 90 76 72 86 56 69 74 91 105 81 97 83 77 87
+85 71 75 99 73 94 98 100 89 110 92 93 95 96 118 112 122 116 114 123 120 106 108 104 124 128 102 101 103 121 115 109 117 111
+119 113 107 125 126 127 129 130 132 131 135 137 138 136 140 134 139 133 142 143 147 144 141 22 188 23 148 149 153 151 150 152
+154 155 156 158 157 182 189 145 160 185 159 146 171 187 173 161 162 163 164 165 166 175 168 167 174 186 172 169 177 178 183
+190 191 192 194 193 179 176 180 181 195 184 196 197 170 198 201 202 205 200 199 204 203 206 207 208 209 210 216 217 211 214
+215 212 219 218 222 224 225 221 213 223 226 231 220 239 240 236 243 232 233 227 228 234 235 229 230 246 251 255 257 261 265
+253 259 241 237 244 242 238 252 258 260 267 263 249 247 268 269 270 275 271 256 262 254 245 266 278 250 264 272 248 279 280
+281 283 284 282 273 274 276 277 287 293 297 295 299 286 301 289 291 303 285 304 309 305 306 290 302 294 300 292 296 298 288
+307 308 313 312 310 311 314 315 316 317 318 319 320 321 322 323 327 325 326 324 328 329 330 331 332 333 334 335 337 338 340
+344 339 345 343 341 336 342 346 347 350 348 351 349 357 356 355 358 361 360 362 359 353 363 375 364 352 365 366 376 377 367
+373 368 374 371 372 369 370 388 384 386 390 379 381 354 382 378 385 387 389 380 383 393 391 392 394 395 398 399 400 401 402
+397 396 403 406 407 404 405 408 409
+""".split()]
 
 
 def _sb(n, d):
@@ -25,39 +42,36 @@ SCRATCH = {
     "uq": _sb(128, X4), "us": _sb(128, U8), "upq": _sb(128, X4), "ups": _sb(128, U8),
     "vq": _sb(128, X4), "vs": _sb(128, U8),
     "wq": _sb(512, X4), "wsc": _sb(512, U8), "zq": _sb(512, X4), "zsc": _sb(512, U8),
-    "xq": _sb(C, X4), "xs": _sb(C, U8),
+    "xq": _sb(C + 2 * K, X4), "xs": _sb(C + 2 * K, U8),
     "zb": _sb(520, BF), "unit": _sb(520, BF),
     "eq": _sb(512, X4), "es": _sb(512, U8),
     "onb": _sb(512, BF), "onq": _sb(128, X4), "ons": _sb(128, U8),
-    "dtb": _sb(512, BF), "dtq": _sb(128, X4), "dts": _sb(128, U8),
+    "dtb": _sb(512, BF), "dtn": _sb(128, BF), "dtq": _sb(128, X4), "dts": _sb(128, U8),
     "onu": _sb(128, BF), "tri": _sb(520, BF), "s1q": _sb(128, X4), "s1s": _sb(128, U8),
     "s2q": _sb(128, X4), "s2s": _sb(128, U8),
-    "pi": _sb(1, I32), "ci": _sb(4, I32), "cf": _sb(4, F32), "c4": _sb(1, F32), "c0": _sb(1, F32), "mr": _sb(4, F32),
-    "m4": _sb(128, BF), "l16": _sb(NB, I32), "ulist": _sb(8, U16), "plist": _sb(HB, U16),
-    "k16": _sb(C, BF), "k4": _sb(4 * TW, BF), "mask16": _sb(H, BF), "keep16": _sb(H, BF), "gate16": _sb(C, BF),
-    "keep4": _sb(4 * TW, BF), "gate4": _sb(K, BF), "cq": _sb(H, F32), "gq": _sb(H, BF), "jv": _sb(C, BF),
-    "m1": _sb(C, F32), "sc": _sb(C, F32), "pex": _sb(C, F32), "pc": _sb(C, F32),
+    "pi": _sb(1, I32), "ci": _sb(4, I32), "cf": _sb(4, F32), "c4": _sb(1, F32), "th": _sb(3, F32), "thb": _sb(2, BF),
+    "m4": _sb(128, BF), "l16": _sb(NB, I32), "ulist": _sb(8, U16),
+    "k16": _sb(H + 16, BF), "k4": _sb(K, BF), "mask16": _sb(H + 16, BF), "keep16": _sb(H, BF),
+    "g4a": _sb(6, BF), "g4b": _sb(4, BF), "g4t": _sb(4, F32), "g4": _sb(C + 8, BF), "tsn": _sb(C + 8, F32), "c5": _sb(4, F32),
+    "gate4": _sb(K, BF), "ga": _sb(H + 18, BF), "gb": _sb(H + 16, BF), "gq": _sb(H + 16, BF), "jv": _sb(C, BF),
+    "m1": _sb(C, F32), "sc": _sb(C, F32), "pc": _sb(C, F32),
     "junk": _sb(16 * HB * (HB - 1) + H, BF),
-    "rs": _sb(NB, F32), "gs": _sb(C, BF), "m2": _sb(C, F16), "sc2": _sb(C, F16), "nn": _sb(NB, F32), "pos": _sb(NB, F32),
-    "aoff": _sb(HB, U16), "moff": _sb(HB, U16), "sa": _sb(C + 8, F32), "fh": _sb(H, BF), "fl": _sb(H, BF), "nl": _sb(H, BF),
+    "f0": _sb(4 * H, BF), "fq0": _sb(H, X4), "fs0": _sb(H, U8), "f1": _sb(4 * H, BF), "fq1": _sb(256, X4), "fs1": _sb(256, U8),
+    "rs": _sb(C, F32), "rx": _sb(NB, F32), "hv": _sb(C, F32), "pos": _sb(NB, F32),
+    "aoff": _sb(HB, U16), "moff": _sb(HB, U16), "sa": _sb(C, F32), "fh": _sb(H, BF), "fl": _sb(H, BF), "nl": _sb(H, BF),
     "nh": _sb(1, F32), "pl": _sb(H, F32),
     "ft": _sb(520, BF), "fq": _sb(130, X4), "fs": _sb(130, U8), "d1": _sb(2 * NB + 1, F32), "nm": _sb(2 * NB + 1, F32),
     "dst": _sb(NB, F32), "doff": _sb(NB, U16),
     "win0": _sb(LOW + K, BF), "win1": _sb(LOW + K, BF),
     "bsn": _sb(K, BF), "boff": _sb(NB, U16), "bt": _sb(512, BF),
     "bq0": _sb(128, X4), "bs0": _sb(128, U8), "bq1": _sb(128, X4), "bs1": _sb(128, U8),
-    "lq": _sb(2 * K + 128, X4), "ls": _sb(2 * K + 128, U8), "ll": _sb(K + 16, BF),
-    "hole": _sb(C, BF), "hs": _sb(C, BF), "ee": _sb(C + 4, BF), "em": _sb(C + 4 * TW + 4, BF), "esn": _sb(8 * TW, BF),
-    "toff": _sb(2 * TW + 2, U16),
-    "tt": _sb(32 * TW, BF), "tq": _sb(2 * (H + 2), X4), "ts": _sb(2 * (H + 2), U8),
-    "osn": _sb(C, BF), "ooff": _sb(NB, U16), "ow": _sb(C, F32), "og": _sb(C, F32), "ob": _sb(C, F32),
+    "ll": _sb(K, BF),
+    "hole": _sb(C, BF), "hs": _sb(C, BF), "ee": _sb(C + 16, BF),
+    "toff": _sb(2 * TW, U16),
+    "tt": _sb(32 * TW, BF), "tq": _sb(4 * H, X4), "ts": _sb(4 * H, U8),
+    "osn": _sb(C + 16, F32), "ooff": _sb(NB, U16), "ow": _sb(C + K, F32), "ob": _sb(C, F32), "cg": _sb(3, F32),
     "yb": _sb(C, F32),
 }
-for _h in range(2):
-    for _i in range(2):
-        SCRATCH["f%d%d" % (_h, _i)] = _sb(4 * H, BF)
-    SCRATCH["fq%d" % _h] = _sb(H + 64 * _h, X4)
-    SCRATCH["fs%d" % _h] = _sb(H + 64 * _h, U8)
 for _i in range(8):
     SCRATCH["ps%d" % _i] = ("psum", [128, 512], F32)
 
@@ -113,33 +127,43 @@ def rank_program(g, core, T, topo):
             writer[k] = tok
             readers[k] = []
 
-    def op(e, call, r=(), w=()):
-        order(e, r, w)
-        cnt[e] += 1
-        call().then_inc(T.sem["s" + e], 1)
-        clock = dict(known[e])
-        clock["s" + e] = cnt[e]
-        note(("s" + e, cnt[e], clock, e), r, w)
+    calls = []
 
-    def dma(e, out, in_, sem, val, r=(), w=()):
-        order(e, r, w)
-        Q[e].dma_start(out, in_).then_inc(T.sem[sem], 16)
-        clock = dict(known[e])
-        clock[sem] = val
-        note((sem, val, clock, "D"), r, w)
+    def op(e, call, r=(), w=()):
+        def issue():
+            order(e, r, w)
+            cnt[e] += 1
+            call().then_inc(T.sem["s" + e], 1)
+            clock = dict(known[e])
+            clock["s" + e] = cnt[e]
+            note(("s" + e, cnt[e], clock, e), r, w)
+        calls.append((e, r, w, issue))
+
+    def dma(e, pairs, sem, r=(), w=()):
+        def issue():
+            order(e, r, w)
+            for out, in_ in pairs:
+                Q[e].dma_start(out, in_).then_inc(T.sem[sem], 16)
+            clock = dict(known[e])
+            clock[sem] = 16 * len(pairs)
+            note((sem, 16 * len(pairs), clock, "D"), r, w)
+        calls.append((e, r, w, issue))
 
     def store(e, out, in_, r):
-        order(e, r, ())
-        Q[e].dma_start(out, in_).then_inc(T.sem.outs, 16)
-        total["outs"] += 16
+        def issue():
+            order(e, r, ())
+            Q[e].dma_start(out, in_).then_inc(T.sem.outs, 16)
+            total["outs"] += 16
+        calls.append((e, r, (), issue))
 
-    def send(out, in_, sem, r):
-        order("G", r, ())
-        g.remote_dma(out, in_, T.sem[sem], T.sem.sent, pid, rid, out_mask)
-        total["sent"] += len(out_e)
-
-    def arrival(key, sem, writes):
-        writer[key] = (sem, writes * len(in_e), {sem: writes * len(in_e)}, "D")
+    def send(pairs, sem, r, key):
+        def issue():
+            order("G", r, ())
+            for out, in_ in pairs:
+                g.remote_dma(out, in_, T.sem[sem], T.sem.sent, pid, rid, out_mask)
+                total["sent"] += len(out_e)
+            writer[key] = (sem, len(pairs) * len(in_e), {sem: len(pairs) * len(in_e)}, "D")
+        calls.append(("G", r, (key,), issue))
 
     V, S = g.vector, g.scalar
 
@@ -186,36 +210,34 @@ def rank_program(g, core, T, topo):
     XC = [T.xc0, T.xc1, T.xc2]
 
     def xk(t, h):
-        return ["x%d.%d.%d" % (t, h, b) for b in range(8)]
+        return ["x%d.%d.%d" % (t, h, b) for b in range(4)]
 
-    dma("Y", T.ub[:], T.u[:], "ldu", 16, w=["ub"])
-    dma("Y", T.xc0[:, 0:4 * H], T.x[:, 0:4 * H], "ldx0", 16, w=xk(0, 0))
-    dma("Y", T.xc0[:, 4 * H:4 * C], T.x[:, 4 * H:4 * C], "ldx1", 16, w=xk(0, 1))
-    order("Y", xk(0, 0) + xk(0, 1), ())
-    g.sync.dma_start(T.wq[:].bitcast(dt.uint8), T.wc[:]).then_inc(T.sem.ldw, 16)
-    g.sync.dma_start(T.zq[:].bitcast(dt.uint8), T.zc[:]).then_inc(T.sem.ldw, 16)
-    g.sync.dma_start(T.wsc[:], T.ws[:]).then_inc(T.sem.ldw, 16)
-    dma("Y", T.zsc[:], T.zs[:], "ldw", 64, w=["wz"])
-    dma("Y", T.vb[:], T.v[:], "ldv", 16, w=["vb"])
+    dma("Y", [(T.ub[:], T.u[:])], "ldu", w=["ub"])
+    dma("Y", [(T.xc0[:, 0:4 * H], T.x[:, 0:4 * H])], "ldx0", w=xk(0, 0))
+    dma("Y", [(T.xc0[:, 4 * H:4 * C], T.x[:, 4 * H:4 * C])], "ldx1", w=xk(0, 1))
+    dma("Y", [(T.wq[:].bitcast(dt.uint8), T.wc[:]), (T.zq[:].bitcast(dt.uint8), T.zc[:]), (T.wsc[:], T.ws[:]), (T.zsc[:], T.zs[:])],
+        "ldw", xk(0, 0) + xk(0, 1), ["wz"])
+    dma("Y", [(T.vb[:], T.v[:])], "ldv", w=["vb"])
 
     iota(T.pi[:], [[0, 1]], 0, 1, ["pi"], small=False)
     iota(T.l16[:], [[16, NB]], 0, 0, ["l16"], small=False)
-    iota(T.m4[:], [[1, 8], [0, 16]], 0, 0, ["m4"])
-    iota(T.k16[:, 0:H], [[0, HB], [1, 16]], 0, 0, ["k16"])
     fill(T.zb[:], 0.0, ["zb"])
+    iota(T.m4[:], [[1, 8], [0, 16]], 0, 0, ["m4"])
+    iota(T.k16[:], [[0, HB + 1], [1, 16]], 0, 0, ["k16"])
     ts(T.ci[:, 0:1], T.pi[:], 4, A.arith_shift_right, r=["pi"], w=["ci0"])
     ts(T.ci[:, 1:2], T.pi[:], 15, A.bitwise_and, r=["pi"], w=["ci1"])
     ts(T.ci[:, 2:3], T.pi[:], 2, A.arith_shift_right, 3, A.bitwise_and, r=["pi"], w=["ci2"])
     ts(T.ci[:, 3:4], T.pi[:], 3, A.bitwise_and, r=["pi"], w=["ci3"])
     vcopy(T.ulist[:], T.l16[:, 0:8], ["l16"], ["ulist"])
     vcopy(T.cf[:], T.ci[:], ["ci0", "ci1", "ci2", "ci3"], ["cf"])
-    ts(T.plist[:], T.l16[:, 0:HB], 15.0, A.add, r=["l16"], w=["plist"])
-    ts(T.onb[:, 0:512:4], T.m4[:], T.cf[:, 0:1], A.is_equal, r=["m4", "cf"], w=["onb.0"])
+    ts(T.onb[:, 0:512:4], T.m4[:], T.cf[:, 0:1], A.is_equal, 1.0 / G, A.mult, r=["m4", "cf"], w=["onb.0"])
     ts(T.onu[:], T.m4[:], T.cf[:, 0:1], A.is_equal, U, A.mult, r=["m4", "cf"], w=["onu"])
-    fill(T.rs[:], 0.0, ["rs%d" % p for p in range(NB)])
-    ts(T.mask16[:], T.k16[:, 0:H], T.cf[:, 1:2], A.is_equal, r=["k16", "cf"], w=["mask16"])
-    ts(T.c0[:], T.cf[:, 1:2], -1023.0, A.mult, r=["cf"], w=["c0"])
-    quant(T.fq1[:, 128:256], T.fs1[:, 128:256], T.zb[:, 0:512], ["zb"], ["qf1"])
+    quant(T.fq1[:, 128:256], T.fs1[:, 128:256], T.zb[:, 0:512], ["zb"], ["qf1", "qf2"])
+    act(T.rs[:, 15:C:H], T.zb[:, 0:2], AF.Copy, ["zb"], ["rs0", "rs1"])
+    ts(T.th[:], T.l16[:, 0:18:K // 16], T.cf[:, 1:2], A.subtract, -0.75, A.add, r=["l16", "cf"], w=["th"])
+    ts(T.mask16[:], T.k16[:], T.cf[:, 1:2], A.is_equal, r=["k16", "cf"], w=["mask16"])
+    for i in range(2):
+        act(T.thb[:, i:i + 1], T.cf[:, 1:2], AF.Identity, ["cf"], ["thb%d" % i], scale=-1.0, bias=143.0 + i)
 
     def sfill(out, width, val, w):
         if val:
@@ -225,52 +247,57 @@ def rank_program(g, core, T, topo):
 
     def slot(p):
         if p == 0 or p > 8:
-            return 0, 0, (12 - p) % 12
-        return 1, (128 if p < 5 else 0), (8 - p) % 4
+            return 0, (12 - p) % 12
+        return (2 if p < 5 else 1), (8 - p) % 4
 
-    def fkeys(h, i):
-        return ["f%d.%d" % (h, p) for p in range(HB) if slot(p)[0] == i]
+    def fkeys(i):
+        return ["f.%d" % p for p in range(HB) if slot(p)[0] == i]
 
-    def zero(h, i):
-        a = 4 * (80 if i else 144)
-        sfill(T["f%d%d" % (h, i)][:, a:4 * H], 4 * H - a, 0.0, fkeys(h, i))
+    def zero(i):
+        a = (576, 320)[i]
+        sfill(T["f%d" % i][:, a:768], 768 - a, 0.0, fkeys(i) + fkeys(2 * i))
 
-    zero(0, 1)
-    zero(0, 0)
+    act(T.onb[:, 60:512:64], T.onb[:, 60:512:64], AF.Copy, ["onb.0"], ["onb.0"], scale=G)
+    act(T.dtn[:], T.onb[:, 0:512:4], AF.Copy, ["onb.0"], ["dtn"], scale=-1.0)
     for t in (1, 2, 3):
         act(T.onb[:, t:512:4], T.onb[:, 0:512:4], AF.Copy, ["onb.0"], ["onb.%d" % t])
-    for t in (1, 2, 3):
-        act(T.dtb[:, t:512:4], T.onb[:, 0:512:4], AF.Copy, ["onb.0"], ["dtb.%d" % t])
-    asel(T.dtb[:, 0:512:4], T.onb[:, 0:512:4], [[1, 128]], A.is_gt, 0, -1, ["onb.0"], ["dtb.0"])
-    iota(T.cq[:], [[-16, HB], [1024, 16]], H - 16, 0, ["cq"])
-    asel(T.sa[:, 0:K + 1], T.zb[:, 0:K + 1], [[0, K + 1]], A.is_gt, -1, 0, ["zb"], ["sa0"], -BIG)
-    asel(T.sa[:, K + H + 1:], T.zb[:, 0:K + 7], [[0, K + 7]], A.is_gt, -1, 0, ["zb"], ["sa"], BIG)
+    asel(T.unit[:], T.zb[:], [[1, 520]], A.not_equal, -3, -4, ["zb"], ["unit"], 1.0)
+    asel(T.dtb[:, 0:512:4], T.dtn[:], [[1, 128]], A.is_gt, 0, -1, ["dtn"], ["dtb.0"])
+    asel(T.sa[:, 0:K], T.zb[:, 0:K], [[0, K]], A.is_gt, -1, 0, ["zb"], ["sa0"], -BIG)
+    asel(T.sa[:, K + H:], T.zb[:, 0:K], [[0, K]], A.is_gt, -1, 0, ["zb"], ["sa1"], BIG)
     for s, (sg, cmp) in enumerate(((1, A.is_ge), (1, A.is_gt), (-1, A.is_gt), (-1, A.is_ge))):
         asel(T.tri[:, s:512:4], T.onu[:], [[sg, 128]], cmp, 0, -sg, ["onu"], ["tri.%d" % s])
     iota(T.jv[:], [[1, C]], -OFF, 0, ["jv"])
-    iota(T.k4[:], [[0, TW], [1, 4]], 0, 0, ["k4"])
-    iota(T.k16[:, H:C], [[0, HB], [1, 16]], 0, 0, ["k16b"])
+    iota(T.k4[:], [[0, NB], [1, 4]], 0, 0, ["k4"])
+    iota(T.ow[:, 0:C], [[1, C]], 0, 0, ["ow0"])
     quant(T.uq[:], T.us[:], T.ub[:], ["ub"], ["uq"])
     act(T.ups[:], T.us[:].indirect(T.ulist[:]), AF.Copy, ["uq", "ulist"], ["ups"])
     vcopy(T.upq[:].bitcast(dt.uint32), T.uq[:].bitcast(dt.uint32).indirect(T.ulist[:]), ["uq", "ulist"], ["upq"])
     act(T.keep16[:], T.k16[:, 0:H], AF.Sign, ["k16"], ["keep16"])
-    zero(1, 1)
-    zero(1, 0)
-    act(T.gq[:], T.cq[:], AF.Abs, ["cq", "c0"], ["gq"], bias=T.c0[:])
+    zero(0)
+    zero(1)
+    for t in (1, 2, 3):
+        act(T.dtb[:, t:512:4], T.onb[:, 0:512:4], AF.Copy, ["onb.0"], ["dtb.%d" % t])
+    act(T.cg[:, 0:1], T.cf[:, 1:2], AF.Copy, ["cf"], ["cg0"], scale=-1.0)
+    sfill(T.ga[:, 0:2], 2, 0.0, ["ga0"])
+    act(T.ga[:, 2:], T.mask16[:], AF.Copy, ["mask16"], ["ga"], scale=G)
+    act(T.gb[:], T.k16[:], AF.Sign, ["k16", "cg0"], ["gb"], bias=T.cg[:, 0:1])
 
     def unit(b):
         quant(T.eq[:, 128 * b:128 * b + 128], T.es[:, 128 * b:128 * b + 128], T.unit[:, 3 - b:515 - b], ["unit"], ["eq%d" % b])
 
+    def state(h):
+        return T.xq[:, K + h * H:K + h * H + H], T.xs[:, K + h * H:K + h * H + H]
+
     def quant_state(t, h):
-        quant(T.xq[:, h * H:h * H + H], T.xs[:, h * H:h * H + H], XC[t][:, 4 * h * H:4 * h * H + 4 * H], xk(t, h), ["xq%d" % h])
+        quant(*state(h), XC[t][:, 4 * h * H:4 * h * H + 4 * H], xk(t, h), ["xq%d" % h])
 
     def scores(h, which=(0, 1)):
         for bank in [4 * h + i for i in which]:
-            mm(PS[bank][:, 0:H], T.upq[:], T.ups[:], T.xq[:, h * H:h * H + H], T.xs[:, h * H:h * H + H], True, True,
-               ["upq", "ups", "xq%d" % h], ["ps%d" % bank])
+            mm(PS[bank][:, 0:H], T.upq[:], T.ups[:], *state(h), True, True, ["upq", "ups", "xq%d" % h], ["ps%d" % bank])
 
     def masked(h):
-        tt(T.m1[:, h * H:h * H + H], PS[4 * h][:, 0:H], T.mask16[:], A.mult, ["ps%d" % (4 * h), "mask16"], ["m1%d" % h])
+        tt(T.m1[:, h * H:h * H + H], PS[4 * h][:, 0:H], T.mask16[:, 0:H], A.mult, ["ps%d" % (4 * h), "mask16"], ["m1%d" % h])
 
     def pivots(h):
         scan(T.sc[:, h * H:h * H + H], T.keep16[:], T.m1[:, h * H:h * H + H], 0.0, A.mult, A.add, ["keep16", "m1%d" % h], ["sc%d" % h])
@@ -278,293 +305,277 @@ def rank_program(g, core, T, topo):
     def keep_scores(h):
         act(T.pc[:, h * H:h * H + H], PS[4 * h + 1][:, 0:H], AF.Copy, ["ps%d" % (4 * h + 1)], ["pc%d" % h])
 
-    def spread(h):
-        act(T.pex[:, h * H:h * H + H], T.sc[:, h * H:h * H + H].indirect(T.plist[:]), AF.Copy, ["sc%d" % h, "plist"], ["pex%d" % h])
-
-    def view(h, p):
-        i, a, s = slot(p)
-        return T["f%d%d" % (h, i)][:, 4 * a + s:4 * (a + (16 * p or H)):4]
+    def view(p):
+        i, s = slot(p)
+        a = 512 * (i == 2)
+        return T["f%d" % min(i, 1)][:, a + s:a + 4 * (16 * p or H):4]
 
     def plane(t, h, p):
-        key, c = "f%d.%d" % (h, p), h * HB + p
+        key, c = "f.%d" % p, h * HB + p
         piv = T.sc[:, 16 * c + 15:16 * c + 16]
         a = 8 * (h * HB * (HB - 1) + p * (p - 1))
-        junk = T.junk[:, a:a + 16 * p]
         if p == 0:
-            tt(view(h, 0), T.pex[:, h * H:h * H + H], PS[4 * h][:, 0:H], A.is_ge, ["pex%d" % h, "ps%d" % (4 * h)], [key])
+            tt(view(0), T.sc[:, h * H:h * H + H], PS[4 * h][:, 0:H], A.is_lt, ["sc%d" % h, "ps%d" % (4 * h)], [key])
         elif p in ON_S[t][h]:
-            act(junk, T.pc[:, h * H:h * H + 16 * p], AF.Sign, ["pc%d" % h, "sc%d" % h], ["j%d" % c], scale=-1.0, bias=piv)
+            act(T.junk[:, a:a + 16 * p], T.pc[:, h * H:h * H + 16 * p], AF.Sign, ["pc%d" % h, "sc%d" % h], ["j%d" % c], scale=-1.0, bias=piv)
         else:
-            ts(view(h, p), PS[4 * h][:, 0:16 * p], piv, A.is_lt, r=["ps%d" % (4 * h), "sc%d" % h], w=[key])
+            ts(view(p), PS[4 * h][:, 0:16 * p], piv, A.is_lt, r=["ps%d" % (4 * h), "sc%d" % h], w=[key])
 
     def rows(t, h, p):
-        key, c = "f%d.%d" % (h, p), h * HB + p
+        key, c = "f.%d" % p, h * HB + p
         a = 8 * (h * HB * (HB - 1) + p * (p - 1))
         junk = T.junk[:, a:a + 16 * p]
         if p in ON_S[t][h]:
-            act(view(h, p), junk, AF.Relu, ["j%d" % c], [key, "rs%d" % c], accum_out=T.rs[:, c:c + 1])
+            act(view(p), junk, AF.Relu, ["j%d" % c], [key, "rx%d" % c], accum_out=T.rx[:, c:c + 1])
         else:
-            act(junk, view(h, p), AF.Copy, [key], ["rs%d" % c, "j%d" % c], accum_out=T.rs[:, c:c + 1])
+            act(junk, view(p), AF.Identity, [key], ["rx%d" % c, "j%d" % c], bias=-1.0, accum_out=T.rs[:, 16 * c + 15:16 * c + 16])
 
-    def pack(h, i):
-        quant(T["fq%d" % i][:, 0:H], T["fs%d" % i][:, 0:H], T["f%d%d" % (h, i)][:], fkeys(h, i), ["qf%d" % i])
+    def rows_less(t, h):
+        d = min(ON_S[t][h])
+        tt(T.rs[:, h * H + 16 * d + 15:h * H + H:16], T.rx[:, h * HB + d:h * HB + HB], T.l16[:, d:HB], A.subtract,
+           ["rx%d" % (h * HB + p) for p in range(d, HB)] + ["l16"], ["rt%d" % h])
+
+    def pack(i):
+        if i == 0:
+            quant(T.fq0[:], T.fs0[:], T.f0[:], fkeys(0), ["qf0"])
+        else:
+            quant(T.fq1[:, 0:H], T.fs1[:, 0:H], T.f1[:], fkeys(1) + fkeys(2), ["qf1", "qf2"])
 
     def columns(h):
-        bank = "ps%d" % (4 * h + 2)
-        mm(PS[4 * h + 2][:, 0:H], T.dtq[:], T.dts[:], T.fq0[:], T.fs0[:], True, False, ["dtq", "qf0"], [bank])
-        for a in (0, 128):
-            mm(PS[4 * h + 2][:, 0:128], T.onq[:], T.ons[:], T.fq1[:, a:a + 128], T.fs1[:, a:a + 128], False, a > 0, ["onq", "qf1"], [bank])
-
-    def inside(h):
-        scan(T.gs[:, h * H:h * H + H], T.gq[:], view(h, 0), 512.0, A.min, A.add, ["gq", "f%d.0" % h], ["gs%d" % h])
-
-    def col_masked(h):
-        tt(T.m2[:, h * H:h * H + H], PS[4 * h + 2][:, 0:H], T.mask16[:], A.mult, ["ps%d" % (4 * h + 2), "mask16"], ["m2%d" % h])
+        out, bank = PS[4 * h + 2], ["ps%d" % (4 * h + 2)]
+        pack(0)
+        mm(out[:, 0:H], T.dtq[:], T.dts[:], T.fq0[:], T.fs0[:], True, False, ["dtq", "qf0"], bank)
+        mm(out[:, 0:H], T.eq[:, 0:128], T.es[:, 0:128], T.fq0[:], T.fs0[:], False, False, ["eq0", "qf0"], bank)
+        pack(1)
+        for i in (1, 2):
+            a = 128 * (i - 1)
+            mm(out[:, 0:128], T.onq[:], T.ons[:], T.fq1[:, a:a + 128], T.fs1[:, a:a + 128], False, i == 2, ["onq", "qf%d" % i], bank)
 
     def col_list(h):
-        scan(T.sc2[:, h * H:h * H + H], T.keep16[:], T.m2[:, h * H:h * H + H], 0.0, A.mult, A.add, ["keep16", "m2%d" % h], ["sc2%d" % h])
+        scan(T.hv[:, h * H:h * H + H], T.gq[:, 0:H], PS[4 * h + 2][:, 0:H], 0.0, A.mult, A.add, ["gq", "ps%d" % (4 * h + 2)], ["hv%d" % h])
 
-    def row_list(h):
-        tt(T.nn[:, h * HB:h * HB + HB], T.gs[:, h * H + 15:h * H + H:16], T.rs[:, h * HB:h * HB + HB], A.add,
-           ["gs%d" % h] + ["rs%d" % (h * HB + p) for p in range(HB)], ["nn%d" % h])
+    def place(h):
+        tt(T.pos[:, h * HB:h * HB + HB], T.hv[:, h * H + 15:h * H + H:16], T.rs[:, h * H + 15:h * H + H:16], A.subtract,
+           ["hv%d" % h, "rs%d" % h, "rt%d" % h] + ["rx%d" % (h * HB + p) for p in range(HB)], ["pos%d" % h])
+
+    def new_state(e, t, h, b):
+        o_, i_ = XC[t][:, 4 * h * H + b:4 * (h + 1) * H:4], PS[4 * h + b][:, 0:H]
+        r, w = ["ps%d" % (4 * h + b)], [xk(t, h)[b]]
+        if e == "V":
+            ts(o_, i_, 0.015625, A.mult, r=r, w=w)
+        else:
+            act(o_, i_, AF.Copy, r, w, scale=0.015625)
 
     quant_state(0, 0)
     scores(0)
     quant(T.onq[:], T.ons[:], T.onb[:], four("onb"), ["onq"])
-    quant(T.dtq[:], T.dts[:], T.dtb[:], four("dtb"), ["dtq"])
 
     for t in range(R):
         last = t == R - 1
         X, win, wk = XC[t], T["win%d" % t], "win%d" % t
         xall = xk(t, 0) + xk(t, 1)
+        on_s = ON_S[t][0]
         masked(0)
         if t == 0:
             quant_state(0, 1)
             scores(1)
         pivots(0)
-        if ON_S[t][0]:
-            keep_scores(0)
-        spread(0)
-        for p in ON_S[t][0]:
+        if t > 0:
+            new_state("S", t, 1, 2)
+            new_state("S", t, 1, 3)
+        keep_scores(0)
+        for p in on_s:
             plane(t, 0, p)
-        for p in range(HB - 1, 0, -1):
-            if p not in ON_S[t][0]:
-                plane(t, 0, p)
+        for p in on_s:
             rows(t, 0, p)
-            if t > 0 and p == 8:
-                quant_state(t, 1)
-                scores(1)
-        masked(1)
+        if t == 0:
+            unit(0)
         plane(t, 0, 0)
+        if t == 0:
+            quant(T.dtq[:], T.dts[:], T.dtb[:], four("dtb"), ["dtq"])
+        for p in range(HB - 1, 0, -1):
+            if p not in on_s:
+                plane(t, 0, p)
+                rows(t, 0, p)
+        if t > 0:
+            quant_state(t, 1)
+            scores(1)
+        masked(1)
+        if t == 0:
+            tt(T.gq[:], T.ga[:, 1:H + 17], T.gb[:], A.max, ["ga", "ga0", "gb"], ["gq"])
         pivots(1)
-        pack(0, 0)
-        pack(0, 1)
         columns(0)
+        on_s = ON_S[t][1]
         keep_scores(1)
-        spread(1)
-        for p in ON_S[t][1]:
+        for p in on_s:
             plane(t, 1, p)
-        for p in ON_S[t][1]:
+        for p in on_s:
             rows(t, 1, p)
-        if not ON_S[t][0]:
-            keep_scores(0)
-        inside(0)
-        mine = [p for p in range(HB - 1, 0, -1) if p not in ON_S[t][1]]
-        for p in mine[:2]:
-            plane(t, 1, p)
-        col_masked(0)
-        plane(t, 1, mine[2])
-        col_list(0)
-        row_list(0)
-        for p in mine[3:]:
-            plane(t, 1, p)
-        for p in mine:
-            rows(t, 1, p)
-        posA, negB = T.pos[:, 0:HB], T.pos[:, HB:NB]
-        tt(posA, T.nn[:, 0:HB], T.sc2[:, 15:H:16], A.subtract, ["nn0", "sc20"], ["posA"])
         plane(t, 1, 0)
-        vcopy(T.aoff[:], posA, ["posA"], ["aoff"])
-        pack(1, 1)
-        pack(1, 0)
+        rows_less(t, 0)
+        for p in range(HB - 1, 0, -1):
+            if p not in on_s:
+                plane(t, 1, p)
+                rows(t, 1, p)
+        col_list(0)
+        place(0)
+        posA, posB = T.pos[:, 0:HB], T.pos[:, HB:NB]
+        th = [T.th[:, i:i + 1] for i in range(3)]
+        ts(T.aoff[:], posA, -1.0, A.mult, th[2], A.add, r=["pos0", "th"], w=["aoff"])
         columns(1)
-        inside(1)
-        vcopy(T.sa[:, K:K + H + 8].indirect(T.aoff[:]), T.pc[:, 0:H], ["pc0", "aoff"], ["sa", "sa0"])
+        vcopy(T.sa[:, K:K + H].indirect(T.aoff[:]), T.pc[:, 0:H], ["pc0", "aoff"], ["sa"])
+        rows_less(t, 1)
         if t == 0:
             sfill(T.tri[:, 512:520], 8, 0.0, ["tri.z"])
             sfill(T.ft[:], 520, 0.0, ["lo0", "lo1", "lp0", "lp1", "hi0", "hi1"])
-        col_masked(1)
-        row_list(1)
         col_list(1)
-        tt(negB, T.sc2[:, H + 15:C:16], T.nn[:, HB:NB], A.subtract, ["nn1", "sc21"], ["negB"])
         if t == 0:
             quant(T.s1q[:], T.s1s[:], T.tri[:, 0:512], four("tri"), ["s1q"])
-        ts(T.moff[:], negB, float(H + 1), A.add, r=["negB"], w=["moff"])
-        act(T.pl[:], T.sa[:, 0:H + 8].indirect(T.moff[:]), AF.Copy, ["sa", "moff"], ["pl"])
-        tt(T.fh[:], T.sa[:, H:].indirect(T.moff[:]), T.pc[:, H:C], A.is_lt, ["sa", "moff", "pc1"], ["fh"])
+        place(1)
+        ts(T.moff[:], posB, th[0], A.subtract, -0.5, A.add, r=["pos1", "th"], w=["moff"])
+        act(T.pl[:], T.sa[:, 0:H].indirect(T.moff[:]), AF.Copy, ["sa", "sa0", "moff"], ["pl"])
+        tt(T.fh[:], T.sa[:, H:].indirect(T.moff[:]), T.pc[:, H:C], A.is_lt, ["sa", "sa1", "moff", "pc1"], ["fh"])
         act(T.junk[:, 16 * HB * (HB - 1):], T.fh[:], AF.Copy, ["fh"], ["nh"], accum_out=T.nh[:])
         tt(T.fl[:], T.pl[:], PS[4][:, 0:H], A.is_lt, ["pl", "ps4"], ["fl"])
         if t == 0:
             quant(T.s2q[:], T.s2s[:], T.tri[:, 2:514], four("tri") + ["tri.z"], ["s2q"])
             sfill(T.d1[:, NB + 1:], NB, 0.0, ["d1z"])
             sfill(win[:], LOW + K, HOLE, [wk])
-            sfill(T.unit[:], 520, 0.0, ["unit"])
-            asel(T.unit[:, 3:515:4], T.onb[:, 0:512:4], [[-1, 128]], A.is_equal, 0, 1, ["onb.0"], ["unit"])
             sfill(T.bt[:, C:512], 512 - C, 0.0, ["bt.z"])
-        scan(T.nl[:], T.fl[:], T.zb[:, 0:H], 0.0, A.add, A.add, ["fl", "zb"], ["nl"])
+        scan(T.nl[:], T.fl[:], T.zb[:, 0:H], -143.75, A.add, A.add, ["fl", "zb"], ["nl"])
         nh, nl = T.nh[:], T.nl[:, H - 1:H]
         o = 16 + 8 * NB
-        ts(T.ft[:, o + 1:o + 8 * HB:8], posA, nh, A.subtract, float(K), A.is_gt, r=["posA", "nh"], w=["hi0"])
-        ts(T.ft[:, o + 1 + 8 * HB:o + 8 * NB:8], negB, nh, A.subtract, -float(H), A.is_lt, r=["negB", "nh"], w=["hi1"])
-        for a, key, ca, cb in ((8, "lo", A.is_le, A.is_ge), (o, "lp", A.is_gt, A.is_lt)):
-            ts(T.ft[:, a:a + 8 * HB:8], posA, nl, A.subtract, -float(K), ca, r=["posA", "nl"], w=[key + "0"])
-            ts(T.ft[:, a + 8 * HB:a + 8 * NB:8], negB, nl, A.subtract, -float(H), cb, r=["negB", "nl"], w=[key + "1"])
+        ts(T.ft[:, o + 1:o + 8 * HB:8], posA, nh, A.add, th[1], A.is_lt, r=["pos0", "nh"], w=["hi0"])
+        ts(T.ft[:, o + 1 + 8 * HB:o + 8 * NB:8], posB, nh, A.subtract, th[0], A.is_lt, r=["pos1", "nh"], w=["hi1"])
+        for a, key, cmp in ((8, "lo", A.is_gt), (o, "lp", A.is_lt)):
+            ts(T.ft[:, a:a + 8 * HB:8], posA, nl, A.add, T.thb[:, 1:2], cmp, r=["pos0", "nl", "thb1"], w=[key + "0"])
+            ts(T.ft[:, a + 8 * HB:a + 8 * NB:8], posB, nl, A.subtract, T.thb[:, 0:1], cmp, r=["pos1", "nl", "thb0"], w=[key + "1"])
         quant(T.fq[:], T.fs[:], T.ft[:], ["lo0", "lo1", "lp0", "lp1", "hi0", "hi1"], ["fq"])
         mm(PS[3][:, 0:128], T.s1q[:], T.s1s[:], T.fq[:, 2:130], T.fs[:, 2:130], True, False, ["s1q", "fq"], ["ps3"])
         mm(PS[3][:, 0:128], T.s2q[:], T.s2s[:], T.fq[:, 0:128], T.fs[:, 0:128], False, True, ["s2q", "fq"], ["ps3"])
         tt(T.d1[:, 0:NB + 1], T.ft[:, 8:o:8], T.ft[:, 0:o - 8:8], A.subtract, ["lo0", "lo1"], ["d1"])
         if t == 0:
-            ts(T.gate4[:], T.k4[:, 0:K], T.cf[:, 2:3], A.is_equal, 2000.0, A.mult, r=["k4", "cf"], w=["gate4"])
+            ts(T.gate4[:], T.k4[:], T.cf[:, 2:3], A.is_equal, 2000.0, A.mult, r=["k4", "cf"], w=["gate4"])
             act(T.gate4[:], T.gate4[:], AF.Identity, ["gate4"], ["gate4"], bias=-1000.0)
-            act(T.keep4[:], T.k4[:], AF.Sign, ["k4"], ["keep4"])
-            ts(T.c4[:], T.cf[:, 3:4], 4.0 * OFF, A.add, r=["cf"], w=["c4"])
-            ts(T.mr[:], T.k4[:, 0:4], T.cf[:, 2:3], A.is_equal, r=["k4", "cf"], w=["mr"])
+            act(T.c4[:], T.cf[:, 3:4], AF.Identity, ["cf"], ["c4"], bias=4.0 * OFF)
         scan(T.nm[:], PS[3][:, 0:4 * NB + 2:2], T.d1[:], (LOW - 1 - 512) * U, A.add, A.add, ["ps3", "d1", "d1z"], ["nm"])
         tt(T.dst[:], T.nm[:, 0:NB], T.nm[:, NB + 1:2 * NB + 1], A.max, ["nm"], ["dst"])
         ts(T.doff[:], T.dst[:], 512.0, A.mult, r=["dst"], w=["doff"])
         vcopy(win[:].indirect(T.doff[:]), T.jv[:], ["jv", "doff"], [wk])
         if last:
-            send(T.ll[:, 16:16 + K], win[:, LOW:LOW + K], "arrl", [wk])
-            arrival("ll", "arrl", 1)
-        scan(T.bsn[:], T.gate4[:], win[:, LOW:LOW + K], 0.0, A.max, A.min, ["gate4", wk], ["bsn"])
+            send([(T.ll[:], win[:, LOW:LOW + K])], "arrl", [wk], "ll")
+        scan(T.bsn[:], T.gate4[:, 0:K], win[:, LOW:LOW + K], 0.0, A.max, A.min, ["gate4", wk], ["bsn"])
         ts(T.boff[:], T.bsn[:, 3:K:4], 4.0, A.mult, T.c4[:], A.add, r=["bsn", "c4"], w=["boff"])
-        act(T.bt[:, 2 * K:4 * K], X[:, 0:4 * C].indirect(T.boff[:, NB // 2:NB]), AF.Copy, xall + ["boff"], ["bt.1"])
-        vcopy(T.bt[:, 0:2 * K], X[:, 0:4 * C].indirect(T.boff[:, 0:NB // 2]), xall + ["boff"], ["bt.0"])
+        act(T.bt[:, 256:4 * K], X[:, 0:4 * C].indirect(T.boff[:, 16:NB]), AF.Copy, xall + ["boff"], ["bt.1"])
+        vcopy(T.bt[:, 0:256], X[:, 0:4 * C].indirect(T.boff[:, 0:16]), xall + ["boff"], ["bt.0"])
         bq, bs = T["bq%d" % t], T["bs%d" % t]
         quant(bq[:], bs[:], T.bt[:], ["bt.0", "bt.1", "bt.z"], ["bq%d" % t])
-        land = t * (K + 128)
-        send(T.lq[:, land:land + K].bitcast(dt.uint8), bq[:, 0:K].bitcast(dt.uint8), "arr%d" % t, ["bq%d" % t])
-        send(T.ls[:, land:land + K], bs[:, 0:K], "arr%d" % t, ["bq%d" % t])
-        arrival("land%d" % t, "arr%d" % t, 2)
-        if last:
-            act(T.ow[:], win[:, 0:C], AF.Identity, [wk], ["ow"], bias=float(OFF))
-        else:
+        land = t * (K + C)
+        send([(T.xq[:, land:land + K].bitcast(dt.uint8), bq[:, 0:K].bitcast(dt.uint8)), (T.xs[:, land:land + K], bs[:, 0:K])],
+             "arr%d" % t, ["bq%d" % t], "land%d" % t)
+        if t == 0:
+            sfill(T.ee[:, C:], 16, 0.0, ["ee2"])
+        act(T.ee[:, C:C + 1], win[:, 0:1], AF.Copy, [wk], ["ee2"])
+        if not last:
             sfill(T.win1[:], LOW + K, HOLE, ["win1"])
-            sfill(T.ll[:, 0:16], 16, -float(OFF), ["ll0"])
-        ts(T.hole[:], win[:, 0:C], 200.0, A.is_gt, r=[wk], w=["hole"])
-        if t == 0:
-            quant(T.lq[:, K:K + 128], T.ls[:, K:K + 128], T.zb[:, 0:512], ["zb"], ["lfill"])
-        scan(T.hs[:], T.hole[:], T.zb[:, 0:C], float(C - 1 - OFF), A.add, A.add, ["hole", "zb"], ["hs"])
-        if t == 0:
-            unit(0)
-        scan(T.ee[:, 0:C], T.hs[:], win[:, 0:C], -1000.0, A.max, A.min, [wk, "hs"], ["ee"])
+        for h in range(2):
+            act(T.hole[:, h * H:h * H + H], win[:, h * H:h * H + H], AF.Relu, [wk], ["hole%d" % h], bias=1.0 - HOLE)
         if t == 0:
             unit(1)
-        else:
-            scan(T.osn[:], T.gate16[:], T.hs[:], 0.0, A.max, A.min, ["gate16", "hs"], ["osn"])
-        vcopy(T.ee[:, C:C + 4], T.ee[:, 0:4], ["ee"], ["ee2"])
-        if t == 0:
             unit(2)
-        else:
-            ts(T.ooff[:], T.osn[:, 15:C:16], float(OFF + 16 - C), A.add, r=["osn"], w=["ooff"])
-        wide = C // 4 + TW + 1
-        for r4 in range(4):
-            a = K * (r4 % 2) + r4 // 2
-            o_, i_ = T.em[:, r4:4 * wide:4], T.ee[:, a:a + 2 * wide - 1:2]
-            if r4 < 2:
-                ts(o_, i_, T.mr[:, r4:r4 + 1], A.mult, r=["ee", "ee2", "mr"], w=["em.%d" % r4])
-            else:
-                act(o_, i_, AF.Copy, ["ee", "ee2", "mr"], ["em.%d" % r4], scale=T.mr[:, r4:r4 + 1])
-        if t == 0:
             unit(3)
-        else:
-            act(T.og[:], T.ll[:].indirect(T.ooff[:]), AF.Identity, ["ll", "ll0", "ooff"], ["og"], bias=float(C + OFF))
-        for h in range(2):
-            scan(T.esn[:, 4 * TW * h:4 * TW * (h + 1)], T.keep4[:], T.em[:, C * h:C * h + 4 * TW], 0.0, A.mult, A.add,
-                 ["keep4"] + four("em"), ["esn%d" % h])
-        for h in range(2):
-            ts(T.toff[:, (TW + 1) * h:(TW + 1) * h + TW], T.esn[:, 4 * TW * h + 3:4 * TW * (h + 1):4], 4.0, A.mult, T.c4[:], A.add,
-               r=["esn%d" % h, "c4"], w=["toff%d" % h])
+        scan(T.hs[:], T.hole[:], T.zb[:, 0:C], float(C - 1 - OFF), A.add, A.add, ["hole0", "hole1", "zb"], ["hs"])
+        scan(T.ee[:, 0:C], T.hs[:], win[:, 0:C], -1000.0, A.max, A.min, [wk, "hs"], ["ee"])
+        if t == 0:
+            ts(T.cg[:, 1:2], T.cf[:, 1:2], 15.0, A.is_lt, 1.0 / G - 1.0, A.mult, r=["cf"], w=["cg1"])
+            quant(T.vq[:], T.vs[:], T.vb[:], ["vb"], ["vq"])
+            ts(T.c5[:, 0:1], T.cf[:, 2:3], 3.0, A.is_lt, 1.0 / G - 1.0, A.mult, r=["cf"], w=["c50"])
+            act(T.c5[:, 1:2], T.c5[:, 0:1], AF.Identity, ["c50"], ["c51"], scale=4.0, bias=4.0)
+            act(T.c5[:, 2:3], T.c4[:], AF.Identity, ["c4"], ["c52"], bias=0.25)
+            sfill(T.g4a[:, 0:2], 2, 0.0, ["g4a0"])
+            act(T.g4a[:, 2:], T.gate4[:, 0:4], AF.Relu, ["gate4"], ["g4a"], scale=G / 1000.0)
+            act(T.c5[:, 3:4], T.cf[:, 2:3], AF.Copy, ["cf"], ["c53"], scale=-1.0)
+            act(T.g4b[:], T.k4[:, 0:4], AF.Sign, ["k4", "c53"], ["g4b"], bias=T.c5[:, 3:4])
+            tt(T.g4t[:], T.g4a[:, 1:5], T.g4b[:], A.max, ["g4a", "g4a0", "g4b"], ["g4t"])
+            for j in range(4):
+                act(T.g4[:, j::4], T.zb[:, 0:K + 2], AF.Identity, ["zb", "g4t"], ["g4.%d" % j], bias=T.g4t[:, j:j + 1])
+            act(T.cg[:, 1:2], T.cg[:, 1:2], AF.Identity, ["cg1"], ["cg1"], bias=1.0)
+        scan(T.tsn[:], T.g4[:], T.ee[:, 0:C + 8], 0.0, A.mult, A.add, four("g4") + ["ee", "ee2"], ["tsn"])
+        ts(T.toff[:, 0:K + 2], T.tsn[:, 3::4], T.c5[:, 1:2], A.mult, T.c5[:, 2:3], A.add, r=["tsn", "c51", "c52"], w=["toff"])
+        if last:
+            for a, b in ((0, H + 16), (H + 16, C)):
+                scan(T.osn[:, a:b], T.gq[:, 0:b - a], T.ee[:, a:b], 0.0, A.mult, A.add, ["gq", "ee"], ["osn%d" % a])
+            ts(T.ooff[:], T.osn[:, 15:C:16], T.cg[:, 1:2], A.mult, OFF + 0.25, A.add, r=["osn0", "osn%d" % (H + 16), "cg1"], w=["ooff"])
+            act(T.ow[:, C:], T.ll[:], AF.Identity, ["ll"], ["ow1"], bias=float(C + OFF))
+            act(T.ob[:], T.ow[:].indirect(T.ooff[:]), AF.Copy, ["ow0", "ow1", "ooff"], ["ob"])
         at, first = (0, 0) if t == 0 else (land + K - 128, 128 - K)
         for b in range(4):
             mm(PS[4 + b][:, 0:128], T.eq[:, 128 * b:128 * b + 128], T.es[:, 128 * b:128 * b + 128],
-               T.lq[:, at:at + 128], T.ls[:, at:at + 128], True, True, ["eq%d" % b, "lfill", "land%d" % t], ["ps%d" % (4 + b)])
+               T.xq[:, at:at + 128], T.xs[:, at:at + 128], True, True, ["eq%d" % b, "xq%d" % t, "land%d" % t], ["ps%d" % (4 + b)])
         for b in range(4):
             o_, i_ = X[:, 4 * C + b:4 * (C + K):4], PS[4 + b][:, first:first + K]
             if b % 2 == 0:
                 act(o_, i_, AF.Copy, ["ps%d" % (4 + b)], ["came%d" % b])
             else:
                 vcopy(o_, i_, ["ps%d" % (4 + b)], ["came%d" % b])
-        src = xall + ["came%d" % b for b in range(4)]
 
         def pick(e, h, a, b):
             o_ = T.tt[:, 16 * (TW * h + a):16 * (TW * h + b)]
-            i_ = X[:].indirect(T.toff[:, (TW + 1) * h + a:(TW + 1) * h + b])
+            i_ = X[:].indirect(T.toff[:, H // 4 * h + a:H // 4 * h + b])
+            r, w = xall + ["came%d" % k for k in range(4)] + ["toff"], ["tt%d%s" % (h, e)]
             if e == "V":
-                vcopy(o_, i_, src + ["toff%d" % h], ["tt%d%s" % (h, e)])
+                vcopy(o_, i_, r, w)
             else:
-                act(o_, i_, AF.Copy, src + ["toff%d" % h], ["tt%d%s" % (h, e)])
+                act(o_, i_, AF.Copy, r, w)
 
-        def quant_t(h):
-            a = h * (H + 2)
-            quant(T.tq[:, a:a + H + 2], T.ts[:, a:a + H + 2], T.tt[:, 16 * TW * h:16 * TW * h + 4 * (H + 2)], ["tt%dV" % h, "tt%dS" % h], ["tq%d" % h])
+        def quant_t(h, z):
+            a, c = H * (2 * h + z), 16 * TW * h + 4 * z
+            quant(T.tq[:, a:a + H], T.ts[:, a:a + H], T.tt[:, c:c + 4 * H], ["tt%dV" % h, "tt%dS" % h], ["tq%d%d" % (h, z)])
 
         def layer(h, banks):
             for b in banks:
                 for z in range(2):
-                    a = h * (H + 2) + 2 * z
+                    a = H * (2 * h + z)
                     wq, ws = (T.zq, T.zsc) if z else (T.wq, T.wsc)
                     mm(PS[4 * h + b][:, 0:H], wq[:, 128 * b:128 * b + 128], ws[:, 128 * b:128 * b + 128],
-                       T.tq[:, a:a + H], T.ts[:, a:a + H], z == 0, z == 1, ["wz", "tq%d" % h], ["ps%d" % (4 * h + b)])
+                       T.tq[:, a:a + H], T.ts[:, a:a + H], z == 0, z == 1, ["wz", "tq%d%d" % (h, z)], ["ps%d" % (4 * h + b)])
 
-        def new_state(e, h, b):
-            for a in range(2):
-                c = 4 * (h * H + a * K)
-                o_, i_ = XC[t + 1][:, c + b:c + 4 * K:4], PS[4 * h + b][:, a:H:2]
-                r, w = ["ps%d" % (4 * h + b)], [xk(t + 1, h)[2 * b + a]]
-                if e == "V":
-                    ts(o_, i_, 0.015625, A.mult, r=r, w=w)
-                else:
-                    act(o_, i_, AF.Copy, r, w, scale=0.015625)
-
-        pick("S", 0, 26, TW)
+        pick("S", 0, 26, TW - 1)
         pick("V", 0, 0, 26)
-        quant_t(0)
+        quant_t(0, 0)
+        quant_t(0, 1)
         layer(0, range(4))
-        pick("S", 1, 26, TW)
-        pick("V", 1, 0, 26)
-        quant_t(1)
-        new_state("S", 0, 0)
-        new_state("V", 0, 1)
-        if t == 0:
-            quant(T.vq[:], T.vs[:], T.vb[:], ["vb"], ["vq"])
-        new_state("S", 0, 2)
-        new_state("V", 0, 3)
+        pick("S", 1, 10, TW - 1)
+        pick("V", 1, 0, 10)
+        quant_t(1, 0)
+        quant_t(1, 1)
+        for b in range(4):
+            new_state("SVSV"[b], t + 1, 0, b)
         quant_state(t + 1, 0)
         layer(1, (0, 1))
         if not last:
             scores(0, (0,))
-            ts(T.gate16[:], T.k16[:], T.cf[:, 1:2], A.is_equal, 2000.0, A.mult, r=["k16", "k16b", "cf"], w=["gate16"])
         layer(1, (2, 3))
         if not last:
             scores(0, (1,))
-        else:
-            scan(T.ob[:], T.og[:], T.ow[:], 0.0, A.max, A.min, ["og", "ow"], ["ob"])
-        for b in range(4):
-            new_state("V" if last and b == 3 else "S", 1, b)
+        for b in range(4 if last else 2):
+            new_state(("SVSV" if last else "SS")[b], t + 1, 1, b)
 
-    store("Y", T.oc[:, 0:4 * H], T.xq[:, 0:H].bitcast(dt.uint8), ["xq0"])
     store("Y", T.ol[:], T.ob[0:128:16, :], ["ob"])
-    mm(PS[0][:, 0:H], T.vq[:], T.vs[:], T.xq[:, 0:H], T.xs[:, 0:H], True, True, ["vq", "xq0"], ["ps0"])
+    store("Y", T.oc[:, 0:4 * H], state(0)[0].bitcast(dt.uint8), ["xq0"])
+    mm(PS[0][:, 0:H], T.vq[:], T.vs[:], *state(0), True, True, ["vq", "xq0"], ["ps0"])
     quant_state(R, 1)
-    mm(PS[1][:, 0:H], T.vq[:], T.vs[:], T.xq[:, H:C], T.xs[:, H:C], True, True, ["vq", "xq1"], ["ps1"])
+    mm(PS[1][:, 0:H], T.vq[:], T.vs[:], *state(1), True, True, ["vq", "xq1"], ["ps1"])
     act(T.yb[:, 0:H], PS[0][:, 0:H], AF.Copy, ["ps0"], ["yb0"])
     store("S", T.y[:, 0:H], T.yb[:, 0:H], ["yb0"])
-    store("Y", T.oc[:, 4 * H:4 * C], T.xq[:, H:C].bitcast(dt.uint8), ["xq1"])
+    store("Y", T.oc[:, 4 * H:4 * C], state(1)[0].bitcast(dt.uint8), ["xq1"])
     for k in range(4):
-        store("Y", T.osc[4 * k:4 * k + 4, :], T.xs[32 * k:32 * k + 4, :], ["xq0", "xq1"])
+        store("Y", T.osc[4 * k:4 * k + 4, :], T.xs[32 * k:32 * k + 4, K:K + C], ["xq0", "xq1"])
     vcopy(T.yb[:, H:C], PS[1][:, 0:H], ["ps1"], ["yb1"])
     store("S", T.y[:, H:C], T.yb[:, H:C], ["yb1"])
 
+    for i in ORDER:
+        calls[i][3]()
     for e in ("V", "S", "P", "G"):
         g.wait_ge(T.sem["s" + e], cnt[e])
     g.wait_ge(T.sem.sent, total["sent"])

from concourse.mybir import dt, AluOpType, ActivationFunctionType

C, K, R = 384, 96, 2
H = C // 2
NB = C // 16
HB = NB // 2
OFF = 240
HOLE = 1024.0
BIG = 9.0e29
U = 1.0 / 512
LOW = 512 - K
TW = 50
G = 131072.0
ON_S = (((11, 10), (11, 10, 9)), ((11,), (11, 10, 9)))

BF, F32, I32, U16, U8, X4 = "bfloat16", "float32", "int32", "uint16", "uint8", "float8_e4m3fn_x4"

ORDER = [int(_x) for _x in """
0 1 2 3 4 7 5 10 12 13 11 6 8 14 18 15 40 16 42 9 53 44 19 45 49 50 41 24 20 21 58 43 25 52 47 54 57 17 55 60 59 61 29 30 37
34 35 38 36 32 33 31 39 88 51 62 26 27 64 48 63 80 68 84 78 46 28 65 66 79 70 82 67 90 76 72 86 56 69 74 91 105 81 97 83 77 87
85 71 75 99 73 94 98 100 89 110 92 93 95 96 118 112 122 116 114 123 120 106 108 104 124 128 102 101 103 121 115 109 117 111
119 113 107 125 126 127 129 130 132 131 135 137 138 136 140 134 139 133 142 143 147 144 141 22 188 23 148 149 153 151 150 152
154 155 156 158 157 182 189 145 160 185 159 146 171 187 173 161 162 163 164 165 166 175 168 167 174 186 172 169 177 178 183
190 191 192 194 193 179 176 180 181 195 184 196 197 170 198 201 202 205 200 199 204 203 206 207 208 209 210 216 217 211 214
215 212 219 218 222 224 225 221 213 223 226 231 220 239 240 236 243 232 233 227 228 234 235 229 230 246 251 255 257 261 265
253 259 241 237 244 242 238 252 258 260 267 263 249 247 268 269 270 275 271 256 262 254 245 266 278 250 264 272 248 279 280
281 283 284 282 273 274 276 277 287 293 297 295 299 286 301 289 291 303 285 304 309 305 306 290 302 294 300 292 296 298 288
307 308 313 312 310 311 314 315 316 317 318 319 320 321 322 323 327 325 326 324 328 329 330 331 332 333 334 335 337 338 340
344 339 345 343 341 336 342 346 347 350 348 351 349 357 356 355 358 361 360 362 359 353 363 375 364 352 365 366 376 377 367
373 368 374 371 372 369 370 388 384 386 390 379 381 354 382 378 385 387 389 380 383 393 391 392 394 395 398 399 400 401 402
397 396 403 406 407 404 405 408 409
""".split()]


def _sb(n, d):
    return ("sbuf", [128, n], d)


SCRATCH = {
    "xc0": _sb(4 * (C + K), BF), "xc1": _sb(4 * (C + K), BF), "xc2": _sb(4 * C, BF),
    "ub": _sb(512, BF), "vb": _sb(512, BF),
    "uq": _sb(128, X4), "us": _sb(128, U8), "upq": _sb(128, X4), "ups": _sb(128, U8),
    "vq": _sb(128, X4), "vs": _sb(128, U8),
    "wq": _sb(512, X4), "wsc": _sb(512, U8), "zq": _sb(512, X4), "zsc": _sb(512, U8),
    "xq": _sb(C + 2 * K, X4), "xs": _sb(C + 2 * K, U8),
    "zb": _sb(520, BF), "unit": _sb(520, BF),
    "eq": _sb(512, X4), "es": _sb(512, U8),
    "onb": _sb(512, BF), "onq": _sb(128, X4), "ons": _sb(128, U8),
    "dtb": _sb(512, BF), "dtn": _sb(128, BF), "dtq": _sb(128, X4), "dts": _sb(128, U8),
    "onu": _sb(128, BF), "tri": _sb(520, BF), "s1q": _sb(128, X4), "s1s": _sb(128, U8),
    "s2q": _sb(128, X4), "s2s": _sb(128, U8),
    "pi": _sb(1, I32), "ci": _sb(4, I32), "cf": _sb(4, F32), "c4": _sb(1, F32), "th": _sb(3, F32), "thb": _sb(2, BF),
    "m4": _sb(128, BF), "l16": _sb(NB, I32), "ulist": _sb(8, U16),
    "k16": _sb(H + 16, BF), "k4": _sb(K, BF), "mask16": _sb(H + 16, BF), "keep16": _sb(H, BF),
    "g4a": _sb(6, BF), "g4b": _sb(4, BF), "g4t": _sb(4, F32), "g4": _sb(C + 8, BF), "tsn": _sb(C + 8, F32), "c5": _sb(4, F32),
    "gate4": _sb(K, BF), "ga": _sb(H + 18, BF), "gb": _sb(H + 16, BF), "gq": _sb(H + 16, BF), "jv": _sb(C, BF),
    "m1": _sb(C, F32), "sc": _sb(C, F32), "pc": _sb(C, F32),
    "junk": _sb(16 * HB * (HB - 1) + H, BF),
    "f0": _sb(4 * H, BF), "fq0": _sb(H, X4), "fs0": _sb(H, U8), "f1": _sb(4 * H, BF), "fq1": _sb(256, X4), "fs1": _sb(256, U8),
    "rs": _sb(C, F32), "rx": _sb(NB, F32), "hv": _sb(C, F32), "pos": _sb(NB, F32),
    "aoff": _sb(HB, U16), "moff": _sb(HB, U16), "sa": _sb(C, F32), "fh": _sb(H, BF), "fl": _sb(H, BF), "nl": _sb(H, BF),
    "nh": _sb(1, F32), "pl": _sb(H, F32),
    "ft": _sb(520, BF), "fq": _sb(130, X4), "fs": _sb(130, U8), "d1": _sb(2 * NB + 1, F32), "nm": _sb(2 * NB + 1, F32),
    "dst": _sb(NB, F32), "doff": _sb(NB, U16),
    "win0": _sb(LOW + K, BF), "win1": _sb(LOW + K, BF),
    "bsn": _sb(K, BF), "boff": _sb(NB, U16), "bt": _sb(512, BF),
    "bq0": _sb(128, X4), "bs0": _sb(128, U8), "bq1": _sb(128, X4), "bs1": _sb(128, U8),
    "ll": _sb(K, BF),
    "hole": _sb(C, BF), "hs": _sb(C, BF), "ee": _sb(C + 16, BF),
    "toff": _sb(2 * TW, U16),
    "tt": _sb(32 * TW, BF), "tq": _sb(4 * H, X4), "ts": _sb(4 * H, U8),
    "osn": _sb(C + 16, F32), "ooff": _sb(NB, U16), "ow": _sb(C + K, F32), "ob": _sb(C, F32), "cg": _sb(3, F32),
    "yb": _sb(C, F32),
}
for _i in range(8):
    SCRATCH["ps%d" % _i] = ("psum", [128, 512], F32)

SEMAPHORES = ["sV", "sS", "sP", "sG", "ldu", "ldx0", "ldx1", "ldw", "ldv", "arr0", "arr1", "arrl", "sent", "outs"]


def rank_program(g, core, T, topo):
    rank = T.rank_of(core)
    if rank is None:
        return
    A, AF = AluOpType, ActivationFunctionType
    n = len(T.cores)
    nxt, prv = T.cores[(rank + 1) % n], T.cores[(rank - 1) % n]
    out_e, in_e = topo.engines(core, nxt), topo.engines(prv, core)
    out_mask = topo.mask(core, nxt)
    rid, pid = topo.addr(nxt)[:2]

    Q = {"V": g.vector, "S": g.scalar, "P": g.tensor, "G": g, "Y": g.sync}
    cnt = {"V": 0, "S": 0, "P": 0, "G": 0}
    known = {e: {} for e in Q}
    writer, readers = {}, {}
    total = {"sent": 0, "outs": 0}

    def need(e, tok):
        sem, val, clock = tok[0], tok[1], tok[2]
        if known[e].get(sem, 0) < val:
            Q[e].wait_ge(T.sem[sem], val)
            for s, v in clock.items():
                known[e][s] = max(known[e].get(s, 0), v)

    def order(e, r, w):
        toks = []
        for k in r:
            if k in writer:
                toks.append(writer[k])
            if k.startswith("ps"):
                toks += [t for t in readers.get(k, []) if t[3] != e]
        for k in w:
            if k in writer and not (e == "P" and writer[k][3] == "P"):
                toks.append(writer[k])
            toks += readers.get(k, [])
        best = {}
        for t in toks:
            if t[0] not in best or best[t[0]][1] < t[1]:
                best[t[0]] = t
        for t in sorted(best.values(), key=lambda t: -len(t[2])):
            need(e, t)

    def note(tok, r, w):
        for k in r:
            readers.setdefault(k, []).append(tok)
        for k in w:
            writer[k] = tok
            readers[k] = []

    calls = []

    def op(e, call, r=(), w=()):
        def issue():
            order(e, r, w)
            cnt[e] += 1
            call().then_inc(T.sem["s" + e], 1)
            clock = dict(known[e])
            clock["s" + e] = cnt[e]
            note(("s" + e, cnt[e], clock, e), r, w)
        calls.append((e, r, w, issue))

    def dma(e, pairs, sem, r=(), w=()):
        def issue():
            order(e, r, w)
            for out, in_ in pairs:
                Q[e].dma_start(out, in_).then_inc(T.sem[sem], 16)
            clock = dict(known[e])
            clock[sem] = 16 * len(pairs)
            note((sem, 16 * len(pairs), clock, "D"), r, w)
        calls.append((e, r, w, issue))

    def store(e, out, in_, r):
        def issue():
            order(e, r, ())
            Q[e].dma_start(out, in_).then_inc(T.sem.outs, 16)
            total["outs"] += 16
        calls.append((e, r, (), issue))

    def send(pairs, sem, r, key):
        def issue():
            order("G", r, ())
            for out, in_ in pairs:
                g.remote_dma(out, in_, T.sem[sem], T.sem.sent, pid, rid, out_mask)
                total["sent"] += len(out_e)
            writer[key] = (sem, len(pairs) * len(in_e), {sem: len(pairs) * len(in_e)}, "D")
        calls.append(("G", r, (key,), issue))

    V, S = g.vector, g.scalar

    def ts(out, in0, s1, o0, s2=None, o1=None, r=(), w=()):
        if o1 is None:
            op("V", lambda: V.tensor_scalar(out, in0, s1, None, o0), r, w)
        else:
            op("V", lambda: V.tensor_scalar(out, in0, s1, s2, o0, o1), r, w)

    def tt(out, a, b, o, r, w):
        op("V", lambda: V.tensor_tensor(out, a, b, o), r, w)

    def scan(out, a, b, init, o0, o1, r, w):
        op("V", lambda: V.tensor_tensor_scan(out, a, b, init, o0, o1), r, w)

    def vcopy(out, in_, r, w):
        op("V", lambda: V.tensor_copy(out, in_), r, w)

    def fill(out, val, w):
        op("V", lambda: V.memset(out, val), (), w)

    def quant(q, s, in_, r, w):
        op("V", lambda: V.quantize_mx(q, s, in_), r, w)

    def act(out, in_, f, r, w, **kw):
        op("S", lambda: S.activation(out, in_, f, **kw), r, w)

    def mm(out, lq, ls, rq, rs, start, stop, r, w):
        op("P", lambda: g.tensor.matmul_mx(out, lq, ls, rq, rs, start, stop), r, w)

    def iota(out, pattern, base, mult, w, small=True):
        if small:
            op("G", lambda: g.iota(out, pattern, base, mult, allow_small_or_imprecise_dtypes=True), (), w)
        else:
            op("G", lambda: g.iota(out, pattern, base, mult), (), w)

    def asel(out, in_, pattern, cmp, base, mult, r, w, other=0.0):
        op("G", lambda: g.affine_select(out, in_, pattern, cmp, other, base, mult), r, w)

    def four(name):
        return ["%s.%d" % (name, t) for t in range(4)]

    PS = [T["ps%d" % i] for i in range(8)]
    XC = [T.xc0, T.xc1, T.xc2]

    def xk(t, h):
        return ["x%d.%d.%d" % (t, h, b) for b in range(4)]

    dma("Y", [(T.ub[:], T.u[:])], "ldu", w=["ub"])
    dma("Y", [(T.xc0[:, 0:4 * H], T.x[:, 0:4 * H])], "ldx0", w=xk(0, 0))
    dma("Y", [(T.xc0[:, 4 * H:4 * C], T.x[:, 4 * H:4 * C])], "ldx1", w=xk(0, 1))
    dma("Y", [(T.wq[:].bitcast(dt.uint8), T.wc[:]), (T.zq[:].bitcast(dt.uint8), T.zc[:]), (T.wsc[:], T.ws[:]), (T.zsc[:], T.zs[:])],
        "ldw", xk(0, 0) + xk(0, 1), ["wz"])
    dma("Y", [(T.vb[:], T.v[:])], "ldv", w=["vb"])

    iota(T.pi[:], [[0, 1]], 0, 1, ["pi"], small=False)
    iota(T.l16[:], [[16, NB]], 0, 0, ["l16"], small=False)
    fill(T.zb[:], 0.0, ["zb"])
    iota(T.m4[:], [[1, 8], [0, 16]], 0, 0, ["m4"])
    iota(T.k16[:], [[0, HB + 1], [1, 16]], 0, 0, ["k16"])
    ts(T.ci[:, 0:1], T.pi[:], 4, A.arith_shift_right, r=["pi"], w=["ci0"])
    ts(T.ci[:, 1:2], T.pi[:], 15, A.bitwise_and, r=["pi"], w=["ci1"])
    ts(T.ci[:, 2:3], T.pi[:], 2, A.arith_shift_right, 3, A.bitwise_and, r=["pi"], w=["ci2"])
    ts(T.ci[:, 3:4], T.pi[:], 3, A.bitwise_and, r=["pi"], w=["ci3"])
    vcopy(T.ulist[:], T.l16[:, 0:8], ["l16"], ["ulist"])
    vcopy(T.cf[:], T.ci[:], ["ci0", "ci1", "ci2", "ci3"], ["cf"])
    ts(T.onb[:, 0:512:4], T.m4[:], T.cf[:, 0:1], A.is_equal, 1.0 / G, A.mult, r=["m4", "cf"], w=["onb.0"])
    ts(T.onu[:], T.m4[:], T.cf[:, 0:1], A.is_equal, U, A.mult, r=["m4", "cf"], w=["onu"])
    quant(T.fq1[:, 128:256], T.fs1[:, 128:256], T.zb[:, 0:512], ["zb"], ["qf1", "qf2"])
    act(T.rs[:, 15:C:H], T.zb[:, 0:2], AF.Copy, ["zb"], ["rs0", "rs1"])
    ts(T.th[:], T.l16[:, 0:18:K // 16], T.cf[:, 1:2], A.subtract, -0.75, A.add, r=["l16", "cf"], w=["th"])
    ts(T.mask16[:], T.k16[:], T.cf[:, 1:2], A.is_equal, r=["k16", "cf"], w=["mask16"])
    for i in range(2):
        act(T.thb[:, i:i + 1], T.cf[:, 1:2], AF.Identity, ["cf"], ["thb%d" % i], scale=-1.0, bias=143.0 + i)

    def sfill(out, width, val, w):
        if val:
            act(out, T.zb[:, 0:width], AF.Identity, ["zb"], w, bias=val)
        else:
            act(out, T.zb[:, 0:width], AF.Copy, ["zb"], w)

    def slot(p):
        if p == 0 or p > 8:
            return 0, (12 - p) % 12
        return (2 if p < 5 else 1), (8 - p) % 4

    def fkeys(i):
        return ["f.%d" % p for p in range(HB) if slot(p)[0] == i]

    def zero(i):
        a = (576, 320)[i]
        sfill(T["f%d" % i][:, a:768], 768 - a, 0.0, fkeys(i) + fkeys(2 * i))

    act(T.onb[:, 60:512:64], T.onb[:, 60:512:64], AF.Copy, ["onb.0"], ["onb.0"], scale=G)
    act(T.dtn[:], T.onb[:, 0:512:4], AF.Copy, ["onb.0"], ["dtn"], scale=-1.0)
    for t in (1, 2, 3):
        act(T.onb[:, t:512:4], T.onb[:, 0:512:4], AF.Copy, ["onb.0"], ["onb.%d" % t])
    asel(T.unit[:], T.zb[:], [[1, 520]], A.not_equal, -3, -4, ["zb"], ["unit"], 1.0)
    asel(T.dtb[:, 0:512:4], T.dtn[:], [[1, 128]], A.is_gt, 0, -1, ["dtn"], ["dtb.0"])
    asel(T.sa[:, 0:K], T.zb[:, 0:K], [[0, K]], A.is_gt, -1, 0, ["zb"], ["sa0"], -BIG)
    asel(T.sa[:, K + H:], T.zb[:, 0:K], [[0, K]], A.is_gt, -1, 0, ["zb"], ["sa1"], BIG)
    for s, (sg, cmp) in enumerate(((1, A.is_ge), (1, A.is_gt), (-1, A.is_gt), (-1, A.is_ge))):
        asel(T.tri[:, s:512:4], T.onu[:], [[sg, 128]], cmp, 0, -sg, ["onu"], ["tri.%d" % s])
    iota(T.jv[:], [[1, C]], -OFF, 0, ["jv"])
    iota(T.k4[:], [[0, NB], [1, 4]], 0, 0, ["k4"])
    iota(T.ow[:, 0:C], [[1, C]], 0, 0, ["ow0"])
    quant(T.uq[:], T.us[:], T.ub[:], ["ub"], ["uq"])
    act(T.ups[:], T.us[:].indirect(T.ulist[:]), AF.Copy, ["uq", "ulist"], ["ups"])
    vcopy(T.upq[:].bitcast(dt.uint32), T.uq[:].bitcast(dt.uint32).indirect(T.ulist[:]), ["uq", "ulist"], ["upq"])
    act(T.keep16[:], T.k16[:, 0:H], AF.Sign, ["k16"], ["keep16"])
    zero(0)
    zero(1)
    for t in (1, 2, 3):
        act(T.dtb[:, t:512:4], T.onb[:, 0:512:4], AF.Copy, ["onb.0"], ["dtb.%d" % t])
    act(T.cg[:, 0:1], T.cf[:, 1:2], AF.Copy, ["cf"], ["cg0"], scale=-1.0)
    sfill(T.ga[:, 0:2], 2, 0.0, ["ga0"])
    act(T.ga[:, 2:], T.mask16[:], AF.Copy, ["mask16"], ["ga"], scale=G)
    act(T.gb[:], T.k16[:], AF.Sign, ["k16", "cg0"], ["gb"], bias=T.cg[:, 0:1])

    def unit(b):
        quant(T.eq[:, 128 * b:128 * b + 128], T.es[:, 128 * b:128 * b + 128], T.unit[:, 3 - b:515 - b], ["unit"], ["eq%d" % b])

    def state(h):
        return T.xq[:, K + h * H:K + h * H + H], T.xs[:, K + h * H:K + h * H + H]

    def quant_state(t, h):
        quant(*state(h), XC[t][:, 4 * h * H:4 * h * H + 4 * H], xk(t, h), ["xq%d" % h])

    def scores(h, which=(0, 1)):
        for bank in [4 * h + i for i in which]:
            mm(PS[bank][:, 0:H], T.upq[:], T.ups[:], *state(h), True, True, ["upq", "ups", "xq%d" % h], ["ps%d" % bank])

    def masked(h):
        tt(T.m1[:, h * H:h * H + H], PS[4 * h][:, 0:H], T.mask16[:, 0:H], A.mult, ["ps%d" % (4 * h), "mask16"], ["m1%d" % h])

    def pivots(h):
        scan(T.sc[:, h * H:h * H + H], T.keep16[:], T.m1[:, h * H:h * H + H], 0.0, A.mult, A.add, ["keep16", "m1%d" % h], ["sc%d" % h])

    def keep_scores(h):
        act(T.pc[:, h * H:h * H + H], PS[4 * h + 1][:, 0:H], AF.Copy, ["ps%d" % (4 * h + 1)], ["pc%d" % h])

    def view(p):
        i, s = slot(p)
        a = 512 * (i == 2)
        return T["f%d" % min(i, 1)][:, a + s:a + 4 * (16 * p or H):4]

    def plane(t, h, p):
        key, c = "f.%d" % p, h * HB + p
        piv = T.sc[:, 16 * c + 15:16 * c + 16]
        a = 8 * (h * HB * (HB - 1) + p * (p - 1))
        if p == 0:
            tt(view(0), T.sc[:, h * H:h * H + H], PS[4 * h][:, 0:H], A.is_lt, ["sc%d" % h, "ps%d" % (4 * h)], [key])
        elif p in ON_S[t][h]:
            act(T.junk[:, a:a + 16 * p], T.pc[:, h * H:h * H + 16 * p], AF.Sign, ["pc%d" % h, "sc%d" % h], ["j%d" % c], scale=-1.0, bias=piv)
        else:
            ts(view(p), PS[4 * h][:, 0:16 * p], piv, A.is_lt, r=["ps%d" % (4 * h), "sc%d" % h], w=[key])

    def rows(t, h, p):
        key, c = "f.%d" % p, h * HB + p
        a = 8 * (h * HB * (HB - 1) + p * (p - 1))
        junk = T.junk[:, a:a + 16 * p]
        if p in ON_S[t][h]:
            act(view(p), junk, AF.Relu, ["j%d" % c], [key, "rx%d" % c], accum_out=T.rx[:, c:c + 1])
        else:
            act(junk, view(p), AF.Identity, [key], ["rx%d" % c, "j%d" % c], bias=-1.0, accum_out=T.rs[:, 16 * c + 15:16 * c + 16])

    def rows_less(t, h):
        d = min(ON_S[t][h])
        tt(T.rs[:, h * H + 16 * d + 15:h * H + H:16], T.rx[:, h * HB + d:h * HB + HB], T.l16[:, d:HB], A.subtract,
           ["rx%d" % (h * HB + p) for p in range(d, HB)] + ["l16"], ["rt%d" % h])

    def pack(i):
        if i == 0:
            quant(T.fq0[:], T.fs0[:], T.f0[:], fkeys(0), ["qf0"])
        else:
            quant(T.fq1[:, 0:H], T.fs1[:, 0:H], T.f1[:], fkeys(1) + fkeys(2), ["qf1", "qf2"])

    def columns(h):
        out, bank = PS[4 * h + 2], ["ps%d" % (4 * h + 2)]
        pack(0)
        mm(out[:, 0:H], T.dtq[:], T.dts[:], T.fq0[:], T.fs0[:], True, False, ["dtq", "qf0"], bank)
        mm(out[:, 0:H], T.eq[:, 0:128], T.es[:, 0:128], T.fq0[:], T.fs0[:], False, False, ["eq0", "qf0"], bank)
        pack(1)
        for i in (1, 2):
            a = 128 * (i - 1)
            mm(out[:, 0:128], T.onq[:], T.ons[:], T.fq1[:, a:a + 128], T.fs1[:, a:a + 128], False, i == 2, ["onq", "qf%d" % i], bank)

    def col_list(h):
        scan(T.hv[:, h * H:h * H + H], T.gq[:, 0:H], PS[4 * h + 2][:, 0:H], 0.0, A.mult, A.add, ["gq", "ps%d" % (4 * h + 2)], ["hv%d" % h])

    def place(h):
        tt(T.pos[:, h * HB:h * HB + HB], T.hv[:, h * H + 15:h * H + H:16], T.rs[:, h * H + 15:h * H + H:16], A.subtract,
           ["hv%d" % h, "rs%d" % h, "rt%d" % h] + ["rx%d" % (h * HB + p) for p in range(HB)], ["pos%d" % h])

    def new_state(e, t, h, b):
        o_, i_ = XC[t][:, 4 * h * H + b:4 * (h + 1) * H:4], PS[4 * h + b][:, 0:H]
        r, w = ["ps%d" % (4 * h + b)], [xk(t, h)[b]]
        if e == "V":
            ts(o_, i_, 0.015625, A.mult, r=r, w=w)
        else:
            act(o_, i_, AF.Copy, r, w, scale=0.015625)

    quant_state(0, 0)
    scores(0)
    quant(T.onq[:], T.ons[:], T.onb[:], four("onb"), ["onq"])

    for t in range(R):
        last = t == R - 1
        X, win, wk = XC[t], T["win%d" % t], "win%d" % t
        xall = xk(t, 0) + xk(t, 1)
        on_s = ON_S[t][0]
        masked(0)
        if t == 0:
            quant_state(0, 1)
            scores(1)
        pivots(0)
        if t > 0:
            new_state("S", t, 1, 2)
            new_state("S", t, 1, 3)
        keep_scores(0)
        for p in on_s:
            plane(t, 0, p)
        for p in on_s:
            rows(t, 0, p)
        if t == 0:
            unit(0)
        plane(t, 0, 0)
        if t == 0:
            quant(T.dtq[:], T.dts[:], T.dtb[:], four("dtb"), ["dtq"])
        for p in range(HB - 1, 0, -1):
            if p not in on_s:
                plane(t, 0, p)
                rows(t, 0, p)
        if t > 0:
            quant_state(t, 1)
            scores(1)
        masked(1)
        if t == 0:
            tt(T.gq[:], T.ga[:, 1:H + 17], T.gb[:], A.max, ["ga", "ga0", "gb"], ["gq"])
        pivots(1)
        columns(0)
        on_s = ON_S[t][1]
        keep_scores(1)
        for p in on_s:
            plane(t, 1, p)
        for p in on_s:
            rows(t, 1, p)
        plane(t, 1, 0)
        rows_less(t, 0)
        for p in range(HB - 1, 0, -1):
            if p not in on_s:
                plane(t, 1, p)
                rows(t, 1, p)
        col_list(0)
        place(0)
        posA, posB = T.pos[:, 0:HB], T.pos[:, HB:NB]
        th = [T.th[:, i:i + 1] for i in range(3)]
        ts(T.aoff[:], posA, -1.0, A.mult, th[2], A.add, r=["pos0", "th"], w=["aoff"])
        columns(1)
        vcopy(T.sa[:, K:K + H].indirect(T.aoff[:]), T.pc[:, 0:H], ["pc0", "aoff"], ["sa"])
        rows_less(t, 1)
        if t == 0:
            sfill(T.tri[:, 512:520], 8, 0.0, ["tri.z"])
            sfill(T.ft[:], 520, 0.0, ["lo0", "lo1", "lp0", "lp1", "hi0", "hi1"])
        col_list(1)
        if t == 0:
            quant(T.s1q[:], T.s1s[:], T.tri[:, 0:512], four("tri"), ["s1q"])
        place(1)
        ts(T.moff[:], posB, th[0], A.subtract, -0.5, A.add, r=["pos1", "th"], w=["moff"])
        act(T.pl[:], T.sa[:, 0:H].indirect(T.moff[:]), AF.Copy, ["sa", "sa0", "moff"], ["pl"])
        tt(T.fh[:], T.sa[:, H:].indirect(T.moff[:]), T.pc[:, H:C], A.is_lt, ["sa", "sa1", "moff", "pc1"], ["fh"])
        act(T.junk[:, 16 * HB * (HB - 1):], T.fh[:], AF.Copy, ["fh"], ["nh"], accum_out=T.nh[:])
        tt(T.fl[:], T.pl[:], PS[4][:, 0:H], A.is_lt, ["pl", "ps4"], ["fl"])
        if t == 0:
            quant(T.s2q[:], T.s2s[:], T.tri[:, 2:514], four("tri") + ["tri.z"], ["s2q"])
            sfill(T.d1[:, NB + 1:], NB, 0.0, ["d1z"])
            sfill(win[:], LOW + K, HOLE, [wk])
            sfill(T.bt[:, C:512], 512 - C, 0.0, ["bt.z"])
        scan(T.nl[:], T.fl[:], T.zb[:, 0:H], -143.75, A.add, A.add, ["fl", "zb"], ["nl"])
        nh, nl = T.nh[:], T.nl[:, H - 1:H]
        o = 16 + 8 * NB
        ts(T.ft[:, o + 1:o + 8 * HB:8], posA, nh, A.add, th[1], A.is_lt, r=["pos0", "nh"], w=["hi0"])
        ts(T.ft[:, o + 1 + 8 * HB:o + 8 * NB:8], posB, nh, A.subtract, th[0], A.is_lt, r=["pos1", "nh"], w=["hi1"])
        for a, key, cmp in ((8, "lo", A.is_gt), (o, "lp", A.is_lt)):
            ts(T.ft[:, a:a + 8 * HB:8], posA, nl, A.add, T.thb[:, 1:2], cmp, r=["pos0", "nl", "thb1"], w=[key + "0"])
            ts(T.ft[:, a + 8 * HB:a + 8 * NB:8], posB, nl, A.subtract, T.thb[:, 0:1], cmp, r=["pos1", "nl", "thb0"], w=[key + "1"])
        quant(T.fq[:], T.fs[:], T.ft[:], ["lo0", "lo1", "lp0", "lp1", "hi0", "hi1"], ["fq"])
        mm(PS[3][:, 0:128], T.s1q[:], T.s1s[:], T.fq[:, 2:130], T.fs[:, 2:130], True, False, ["s1q", "fq"], ["ps3"])
        mm(PS[3][:, 0:128], T.s2q[:], T.s2s[:], T.fq[:, 0:128], T.fs[:, 0:128], False, True, ["s2q", "fq"], ["ps3"])
        tt(T.d1[:, 0:NB + 1], T.ft[:, 8:o:8], T.ft[:, 0:o - 8:8], A.subtract, ["lo0", "lo1"], ["d1"])
        if t == 0:
            ts(T.gate4[:], T.k4[:], T.cf[:, 2:3], A.is_equal, 2000.0, A.mult, r=["k4", "cf"], w=["gate4"])
            act(T.gate4[:], T.gate4[:], AF.Identity, ["gate4"], ["gate4"], bias=-1000.0)
            act(T.c4[:], T.cf[:, 3:4], AF.Identity, ["cf"], ["c4"], bias=4.0 * OFF)
        scan(T.nm[:], PS[3][:, 0:4 * NB + 2:2], T.d1[:], (LOW - 1 - 512) * U, A.add, A.add, ["ps3", "d1", "d1z"], ["nm"])
        tt(T.dst[:], T.nm[:, 0:NB], T.nm[:, NB + 1:2 * NB + 1], A.max, ["nm"], ["dst"])
        ts(T.doff[:], T.dst[:], 512.0, A.mult, r=["dst"], w=["doff"])
        vcopy(win[:].indirect(T.doff[:]), T.jv[:], ["jv", "doff"], [wk])
        if last:
            send([(T.ll[:], win[:, LOW:LOW + K])], "arrl", [wk], "ll")
        scan(T.bsn[:], T.gate4[:, 0:K], win[:, LOW:LOW + K], 0.0, A.max, A.min, ["gate4", wk], ["bsn"])
        ts(T.boff[:], T.bsn[:, 3:K:4], 4.0, A.mult, T.c4[:], A.add, r=["bsn", "c4"], w=["boff"])
        act(T.bt[:, 256:4 * K], X[:, 0:4 * C].indirect(T.boff[:, 16:NB]), AF.Copy, xall + ["boff"], ["bt.1"])
        vcopy(T.bt[:, 0:256], X[:, 0:4 * C].indirect(T.boff[:, 0:16]), xall + ["boff"], ["bt.0"])
        bq, bs = T["bq%d" % t], T["bs%d" % t]
        quant(bq[:], bs[:], T.bt[:], ["bt.0", "bt.1", "bt.z"], ["bq%d" % t])
        land = t * (K + C)
        send([(T.xq[:, land:land + K].bitcast(dt.uint8), bq[:, 0:K].bitcast(dt.uint8)), (T.xs[:, land:land + K], bs[:, 0:K])],
             "arr%d" % t, ["bq%d" % t], "land%d" % t)
        if t == 0:
            sfill(T.ee[:, C:], 16, 0.0, ["ee2"])
        act(T.ee[:, C:C + 1], win[:, 0:1], AF.Copy, [wk], ["ee2"])
        if not last:
            sfill(T.win1[:], LOW + K, HOLE, ["win1"])
        for h in range(2):
            act(T.hole[:, h * H:h * H + H], win[:, h * H:h * H + H], AF.Relu, [wk], ["hole%d" % h], bias=1.0 - HOLE)
        if t == 0:
            unit(1)
            unit(2)
            unit(3)
        scan(T.hs[:], T.hole[:], T.zb[:, 0:C], float(C - 1 - OFF), A.add, A.add, ["hole0", "hole1", "zb"], ["hs"])
        scan(T.ee[:, 0:C], T.hs[:], win[:, 0:C], -1000.0, A.max, A.min, [wk, "hs"], ["ee"])
        if t == 0:
            ts(T.cg[:, 1:2], T.cf[:, 1:2], 15.0, A.is_lt, 1.0 / G - 1.0, A.mult, r=["cf"], w=["cg1"])
            quant(T.vq[:], T.vs[:], T.vb[:], ["vb"], ["vq"])
            ts(T.c5[:, 0:1], T.cf[:, 2:3], 3.0, A.is_lt, 1.0 / G - 1.0, A.mult, r=["cf"], w=["c50"])
            act(T.c5[:, 1:2], T.c5[:, 0:1], AF.Identity, ["c50"], ["c51"], scale=4.0, bias=4.0)
            act(T.c5[:, 2:3], T.c4[:], AF.Identity, ["c4"], ["c52"], bias=0.25)
            sfill(T.g4a[:, 0:2], 2, 0.0, ["g4a0"])
            act(T.g4a[:, 2:], T.gate4[:, 0:4], AF.Relu, ["gate4"], ["g4a"], scale=G / 1000.0)
            act(T.c5[:, 3:4], T.cf[:, 2:3], AF.Copy, ["cf"], ["c53"], scale=-1.0)
            act(T.g4b[:], T.k4[:, 0:4], AF.Sign, ["k4", "c53"], ["g4b"], bias=T.c5[:, 3:4])
            tt(T.g4t[:], T.g4a[:, 1:5], T.g4b[:], A.max, ["g4a", "g4a0", "g4b"], ["g4t"])
            for j in range(4):
                act(T.g4[:, j::4], T.zb[:, 0:K + 2], AF.Identity, ["zb", "g4t"], ["g4.%d" % j], bias=T.g4t[:, j:j + 1])
            act(T.cg[:, 1:2], T.cg[:, 1:2], AF.Identity, ["cg1"], ["cg1"], bias=1.0)
        scan(T.tsn[:], T.g4[:], T.ee[:, 0:C + 8], 0.0, A.mult, A.add, four("g4") + ["ee", "ee2"], ["tsn"])
        ts(T.toff[:, 0:K + 2], T.tsn[:, 3::4], T.c5[:, 1:2], A.mult, T.c5[:, 2:3], A.add, r=["tsn", "c51", "c52"], w=["toff"])
        if last:
            for a, b in ((0, H + 16), (H + 16, C)):
                scan(T.osn[:, a:b], T.gq[:, 0:b - a], T.ee[:, a:b], 0.0, A.mult, A.add, ["gq", "ee"], ["osn%d" % a])
            ts(T.ooff[:], T.osn[:, 15:C:16], T.cg[:, 1:2], A.mult, OFF + 0.25, A.add, r=["osn0", "osn%d" % (H + 16), "cg1"], w=["ooff"])
            act(T.ow[:, C:], T.ll[:], AF.Identity, ["ll"], ["ow1"], bias=float(C + OFF))
            act(T.ob[:], T.ow[:].indirect(T.ooff[:]), AF.Copy, ["ow0", "ow1", "ooff"], ["ob"])
        at, first = (0, 0) if t == 0 else (land + K - 128, 128 - K)
        for b in range(4):
            mm(PS[4 + b][:, 0:128], T.eq[:, 128 * b:128 * b + 128], T.es[:, 128 * b:128 * b + 128],
               T.xq[:, at:at + 128], T.xs[:, at:at + 128], True, True, ["eq%d" % b, "xq%d" % t, "land%d" % t], ["ps%d" % (4 + b)])
        for b in range(4):
            o_, i_ = X[:, 4 * C + b:4 * (C + K):4], PS[4 + b][:, first:first + K]
            if b % 2 == 0:
                act(o_, i_, AF.Copy, ["ps%d" % (4 + b)], ["came%d" % b])
            else:
                vcopy(o_, i_, ["ps%d" % (4 + b)], ["came%d" % b])

        def pick(e, h, a, b):
            o_ = T.tt[:, 16 * (TW * h + a):16 * (TW * h + b)]
            i_ = X[:].indirect(T.toff[:, H // 4 * h + a:H // 4 * h + b])
            r, w = xall + ["came%d" % k for k in range(4)] + ["toff"], ["tt%d%s" % (h, e)]
            if e == "V":
                vcopy(o_, i_, r, w)
            else:
                act(o_, i_, AF.Copy, r, w)

        def quant_t(h, z):
            a, c = H * (2 * h + z), 16 * TW * h + 4 * z
            quant(T.tq[:, a:a + H], T.ts[:, a:a + H], T.tt[:, c:c + 4 * H], ["tt%dV" % h, "tt%dS" % h], ["tq%d%d" % (h, z)])

        def layer(h, banks):
            for b in banks:
                for z in range(2):
                    a = H * (2 * h + z)
                    wq, ws = (T.zq, T.zsc) if z else (T.wq, T.wsc)
                    mm(PS[4 * h + b][:, 0:H], wq[:, 128 * b:128 * b + 128], ws[:, 128 * b:128 * b + 128],
                       T.tq[:, a:a + H], T.ts[:, a:a + H], z == 0, z == 1, ["wz", "tq%d%d" % (h, z)], ["ps%d" % (4 * h + b)])

        pick("S", 0, 26, TW - 1)
        pick("V", 0, 0, 26)
        quant_t(0, 0)
        quant_t(0, 1)
        layer(0, range(4))
        pick("S", 1, 10, TW - 1)
        pick("V", 1, 0, 10)
        quant_t(1, 0)
        quant_t(1, 1)
        for b in range(4):
            new_state("SVSV"[b], t + 1, 0, b)
        quant_state(t + 1, 0)
        layer(1, (0, 1))
        if not last:
            scores(0, (0,))
        layer(1, (2, 3))
        if not last:
            scores(0, (1,))
        for b in range(4 if last else 2):
            new_state(("SVSV" if last else "SS")[b], t + 1, 1, b)

    store("Y", T.ol[:], T.ob[0:128:16, :], ["ob"])
    store("Y", T.oc[:, 0:4 * H], state(0)[0].bitcast(dt.uint8), ["xq0"])
    mm(PS[0][:, 0:H], T.vq[:], T.vs[:], *state(0), True, True, ["vq", "xq0"], ["ps0"])
    quant_state(R, 1)
    mm(PS[1][:, 0:H], T.vq[:], T.vs[:], *state(1), True, True, ["vq", "xq1"], ["ps1"])
    act(T.yb[:, 0:H], PS[0][:, 0:H], AF.Copy, ["ps0"], ["yb0"])
    store("S", T.y[:, 0:H], T.yb[:, 0:H], ["yb0"])
    store("Y", T.oc[:, 4 * H:4 * C], state(1)[0].bitcast(dt.uint8), ["xq1"])
    for k in range(4):
        store("Y", T.osc[4 * k:4 * k + 4, :], T.xs[32 * k:32 * k + 4, K:K + C], ["xq0", "xq1"])
    vcopy(T.yb[:, H:C], PS[1][:, 0:H], ["ps1"], ["yb1"])
    store("S", T.y[:, H:C], T.yb[:, H:C], ["yb1"])

    for i in ORDER:
        calls[i][3]()
    for e in ("V", "S", "P", "G"):
        g.wait_ge(T.sem["s" + e], cnt[e])
    g.wait_ge(T.sem.sent, total["sent"])
    g.wait_ge(T.sem.outs, total["outs"])
